import numpy as np, ml_dtypes
CORES = [3,7,11,15,131,135,139,143]
N = 8
import mx_ref
BF = ml_dtypes.bfloat16
def gentries(a):
    return np.ascontiguousarray(a.reshape(8, 16, -1).transpose(0, 2, 1)).reshape(8, -1)
def gtable(e):
    e = np.asarray(e); return np.ascontiguousarray(e.reshape(8, -1, 16).transpose(0, 2, 1)).reshape(128, -1).astype(np.int32)
def gcols(t, e):
    v = np.concatenate([t.reshape(8, 16, -1, 4), np.zeros((8, 16, 1, 4), BF)], axis=2)
    return np.ascontiguousarray(np.stack([v[g][:, e[g]] for g in range(8)])).reshape(128, -1)
def tile(rs):
    return np.stack(rs, axis=2).reshape(128, -1).astype(BF)
def pick(q, e):
    c = np.concatenate([q[0].reshape(128, -1, 4), np.zeros((128, 1, 4), np.uint8)], axis=1); s = np.concatenate([q[1], np.ones((16, 1), np.uint8)], axis=1)
    return (np.ascontiguousarray(c[:, e].reshape(128, -1)), np.ascontiguousarray(s[:, e]))
def join(*qs):
    return (np.concatenate([q[0] for q in qs], axis=1), np.concatenate([q[1] for q in qs], axis=1))
def put(q, e, v):
    c, s = q[0].reshape(128, -1, 4).copy(), q[1].copy(); c[:, e] = v[0].reshape(128, -1, 4); s[:, e] = v[1]
    return (c.reshape(128, -1), s)
def pk(c, s):
    return (np.ascontiguousarray(c), mx_ref.live(s))
def emit(q):
    return q[0], q[1]
def packed(v, rng):
    q = [mx_ref.quantize(np.ascontiguousarray(v[r])) for r in range(N)]
    return np.stack([a for a, b in q]), np.stack([mx_ref.plane(b, rng) for a, b in q])
def values_of_codes():
    e, c = np.zeros((128, 128, 4), np.float32), np.zeros((128, 2, 4), np.uint8)
    e[np.arange(128), np.arange(128), 0] = 1
    c[:127, :, 0] = np.arange(256).reshape(2, 128).T[:127]
    return mx_ref.matmul(mx_ref.quantize(e.reshape(128, 512).astype(BF)), (c.reshape(128, 8), np.full((16, 2), 127, np.uint8))).T.reshape(-1).astype(np.float64)
CODE_VALUE, SCALE_VALUE = values_of_codes(), 2.0 ** (np.arange(256) - 127.0)
def decode(q):
    return (CODE_VALUE[q[0]].reshape(16, 8, -1, 4) * SCALE_VALUE[q[1]][:, None, :, None] + 0.0).reshape(128, -1).astype(np.float32)
def f(rng, *shape):
    return mx_ref.flush((rng.standard_normal(shape, dtype=np.float32) * np.exp2(rng.integers(-2, 3, shape[:-1] + (1,)))).astype(BF))
def wide(rng, *shape, cols=0):
    v = rng.standard_normal(shape, dtype=np.float32) * np.exp2(rng.integers(-12, 13, shape)).astype(np.float32)
    if cols: v *= np.repeat(np.exp2(rng.integers(-cols, cols + 1, shape[:-2] + (1, shape[-1] // 4))) * (rng.random(shape[:-2] + (1, shape[-1] // 4)) > 0.0625), 4, axis=-1).astype(np.float32)
    return mx_ref.flush(v.astype(BF))
C, B, R = 256, 7, 3
K = 1 << B
def items(p):
    return np.sum((p.reshape(8, 16, -1)[:, :B] + np.float32(0.0) < 0) * (1 << np.arange(B))[:, None], axis=1)
def distances(a, n):
    last = K - 1 - np.argsort(a, axis=2)
    d = np.zeros((N, 8, C), np.int64)
    for j in range(C):
        i = n[:, :, j:j + 1]
        d[:, :, j] = np.sum(last > np.take_along_axis(last, i, axis=2), axis=2)
        np.put_along_axis(last, i, K + j, axis=2)
    return d, last
def big(v):
    v = v.astype(np.float32)
    v[np.abs(v) < np.float32(2.0 ** -16)] = 0
    return v.astype(BF)
def fronts(rng):
    return np.argsort(rng.random((N, 8, K)), axis=2)
def stored(a):
    return np.stack([gtable(e) for e in a])
def numbers_of(rng):
    return {"x": big(f(rng, N, 128, 4 * C)), "h": big(f(rng, N, 128, 4 * K)), "nm": stored(fronts(rng)), "u": np.array(f(rng, N, 128, 512)), "v": np.array(f(rng, N, 128, 512))}
def layers(w, rng):
    c, p = packed(np.ascontiguousarray(w).reshape(N, 128, 2048), rng)
    return {"wc": c, "ws": p}
def weights(rng, q=-1):
    w = np.array(f(rng, N, 128, 2048)).reshape(N, 128, 4, 128, 4)
    if q >= 0:
        w[:, 16 * q:16 * q + 16] = 0
        for i in range(16 * q, 16 * q + 16):
            w[:, :, :, i] = 0
            for b in range(4): w[:, i, b, i, b] = 64
    return layers(w, rng)
def seven(c, rng):
    j = np.arange(C)
    a = j % (2 * K)
    return [c[j % K], c[np.minimum(a, 2 * K - 1 - a)], c[rng.integers(0, 3, C)], c[8 * j // C], np.full(C, K - 1), rng.integers(0, K, C), rng.integers(0, K // 2, C)]
def setup_inputs(rng):
    return {**numbers_of(rng), **weights(rng)}
def setup_inputs_traces(rng):
    d, nm = numbers_of(rng), fronts(rng)
    q = int(rng.integers(8))
    size = np.exp2(np.array([-29.0, -12.0, 0.0, 10.0])[rng.permutation(N) % 4])
    x, h = d["x"].reshape(N, 128, C, 4), d["h"].reshape(N, 128, K, 4)
    x[:, 16 * q:16 * q + 16] = 0
    h[:, 16 * q:16 * q + 16] = 0
    u = d["u"].reshape(N, 128, 8, 16, 4)
    u[:, :, :, :B] = 0
    rest = np.delete(np.arange(8), q)
    k = np.arange(7 * B)
    for r in range(N):
        n = np.zeros((8, C), np.int64)
        for i, g in enumerate(rng.permutation(rest)): n[g] = seven(nm[r, g][::-1], rng)[i]
        digit = (n[rest][:, None] >> np.arange(B)[:, None]) & 1
        mark = np.zeros((64, C))
        mark[:7 * B] = np.where(digit == 1, -1, rng.integers(0, 2, digit.shape)).reshape(7 * B, C) * size[r]
        mark[:, C - 1] = 0
        x[r, 16 * q:16 * q + 16] = mark.reshape(16, 4, C).transpose(0, 2, 1).astype(np.float32).astype(BF)
        u[r, 16 * q + k // 4, rest[k // B], k % B, k % 4] = 2.0 ** -30 if size[r] < 2.0 ** -20 else 1.0
    return {"x": x.reshape(N, 128, 4 * C), "h": h.reshape(N, 128, 4 * K), "nm": stored(nm), "u": u.reshape(N, 128, 512), "v": d["v"], **weights(rng, q)}
def setup_inputs_copies(rng):
    d = setup_inputs(rng)
    o = rng.permutation(N)
    x = d["x"].reshape(N, 128, C, 4)
    for r in range(N): x[r] = x[r][:, rng.integers(0, 1 + 2 * o[r], C)]
    x[o == 1] = 0
    d["x"] = x.reshape(N, 128, 4 * C)
    return d
def setup_inputs_huge(rng):
    d = numbers_of(rng)
    o = rng.permutation(N)
    s = rng.choice([-1.0, 1.0], (N, 8, C))
    s[o == 0] = -1
    s[o == 1] = 1
    x = 2.0 ** 30 * (0.75 + 0.25 * rng.random((N, 128, C, 4))) * np.tile(s, (1, 16, 1))[:, :, :, None]
    h = 2.0 ** 28 * (0.75 + 0.25 * rng.random((N, 128, 4 * K))) * rng.choice([-1.0, 1.0], (N, 128, 4 * K))
    on = (np.arange(128)[:, None, None] % 8 == np.argsort(rng.random((8, 8)), axis=1)[:, :B]) | (o < 2)[:, None, None, None]
    u = d["u"].reshape(N, 128, 8, 16, 4)
    u[:, :, :, :B] = (2.0 ** 30 * (0.75 + 0.25 * rng.random((N, 128, 8, B, 4))) * on[:, :, :, :, None]).astype(np.float32).astype(BF)
    w = np.zeros((N, 128, 4, 128, 4), np.float32)
    i = np.arange(128)
    for b in range(4): w[:, i, b, i, b] = 32
    return {"x": x.astype(np.float32).reshape(N, 128, 4 * C).astype(BF), "h": h.astype(np.float32).astype(BF), "nm": d["nm"], "u": u.reshape(N, 128, 512), "v": d["v"], **layers(w.astype(BF), rng)}
def setup_inputs_spread(rng):
    d = setup_inputs(rng)
    d["x"] = big(wide(rng, N, 128, 4 * C, cols=6))
    d["h"] = big(wide(rng, N, 128, 4 * K, cols=6))
    return d
def check_inputs(d):
    b = []
    for k in ("x", "h", "u", "v"):
        a = np.abs(d[k].astype(np.float32))
        if not (np.isfinite(a).all() and ((a == 0) | (a >= 2.0 ** -30) & (a <= 2.0 ** 30)).all()): b.append("a value of " + k)
    if any((np.sort(gentries(d["nm"][r]), axis=1) != np.arange(K)).any() for r in range(N)): b.append("nm: a group's entries aren't a permutation")
    return b
def reference(x, h, nm, u, v, wc, ws):
    qu = [mx_ref.quantize(u[r]) for r in range(N)]
    lay = [pk(wc[r], ws[r]) for r in range(N)]
    qx = [mx_ref.quantize(x[r]) for r in range(N)]
    qf = [mx_ref.quantize(h[r]) for r in range(N)]
    a = np.stack([gentries(nm[r]) for r in range(N)]).astype(np.int64)
    for t in range(R):
        d, last = distances(a, np.stack([items(mx_ref.matmul(qu[r], qx[r])) for r in range(N)]))
        m = np.argsort(-last, axis=2, kind="stable")
        s = np.take_along_axis(last, m, axis=2)
        border = []
        for r in range(N):
            own, front = decode(qx[r]).astype(BF), decode(qf[r]).astype(BF)
            z = ((own.astype(np.float32) + gcols(front, d[r]).astype(np.float32)) * np.float32(0.5)).astype(BF)
            q = mx_ref.quantize(z)
            qx[r] = mx_ref.quantize(tile([mx_ref.matmul(pick(lay[r], np.arange(128 * b, 128 * b + 128)), q) * np.float32(0.03125) for b in range(4)]))
            both = np.concatenate([decode(qx[r]).astype(BF), front], axis=1)
            border.append(mx_ref.quantize(gcols(both, np.where(s[r] >= K, s[r] - K, C + K - 1 - s[r]))))
        qf = [border[(r - 1) % N] for r in range(N)]
        a = np.stack([m[(r - 1) % N] for r in range(N)])
    y, ol = np.zeros((N, 128, C + K), np.float32), np.zeros((N, 8, C + K), np.float32)
    oc, osc = np.zeros((N, 128, 4 * (C + K)), np.uint8), np.zeros((N, 16, C + K), np.uint8)
    for r in range(N):
        q = join(qx[r], qf[r])
        y[r] = mx_ref.matmul(mx_ref.quantize(v[r]), q)
        ol[r] = np.concatenate([d[r], a[r]], axis=1)
        oc[r], osc[r] = emit(q)
    return {"y": y, "ol": ol, "oc": oc, "osc": osc}

@@ -1,0 +1,509 @@
+from concourse.mybir import dt, AluOpType as A, ActivationFunctionType as F, AxisListType
+
+C, K, R = 256, 128, 3
+MS = 11
+NMID = 7
+NEARLY = 5
+NLAST = 4
+LSTEP = 9
+YV = 3
+HALF = 0.5
+
+
+def off1(m):
+    return 8 * m * (m + 1)
+
+
+def off2(m):
+    return 256 + 16 * MS * (m - 1) if 2 * m <= MS else 256 + 16 * MS * (MS - m - 1) + 16 * (MS - m)
+
+
+S2 = 256 + 8 * MS * (MS - 1)
+BF, F32, I32, U16, U8, Q8 = "bfloat16", "float32", "int32", "uint16", "uint8", "float8_e4m3fn_x4"
+SCRATCH, TINY = {}, {}
+
+
+def buf(name, n, d=BF, where="sbuf"):
+    SCRATCH[name] = (where, [128, n], d)
+
+
+for _n, _w in (("xin", 1024), ("hin", 512), ("uin", 512), ("vin", 512), ("bits", 512), ("ctile", 2048), ("ntile", 1024),
+               ("zt", 1024), ("yt", 1024), ("blk", 128), ("idn", 128), ("o16", 16), ("pe16", 16), ("r16", 256), ("diag", 256),
+               ("keep", 256), ("keep2", S2), ("tmpl", 272), ("own1", 16), ("own2", 16), ("inc", 2176), ("iota", 384), ("plc", 128),
+               ("plcr", 128), ("zeros", 256), ("ones", 384), ("hm", 256), ("hold", 256), ("qq", 2176), ("sc", 2176), ("pl", 256),
+               ("plh", 256), ("vr", 256), ("vw", 16), ("lt", S2), ("sc2", S2 + 16), ("junk", 1536), ("ltb", 816), ("cs", 2176),
+               ("mn", 128), ("mh", 128), ("arow", 384), ("gx", 1536)):
+    buf(_n, _w)
+for _n, _w in (("kap", 1), ("pw", 1), ("k1", 1), ("k2", 1), ("e1", 1), ("e2", 1), ("e3", 1), ("pe", 1), ("sel1", 1), ("sel2", 1), ("pr", 1),
+               ("base", 16), ("base0", 16), ("thr", 8), ("pwv", 16),
+               ("thr0", 8), ("thrl", 8), ("x1", 16), ("nh", 16), ("w1", 16), ("w", 16), ("acc", 16), ("e32", 32), ("dd", 16), ("d", 16), ("accb", 8),
+               ("sa_", 8), ("sb_", 8), ("sc_", 8), ("sf_", 8), ("c2", 8), ("c2l", 8), ("b127", 1), ("bm64", 1)):
+    TINY[_n] = (sum(w for o, w in TINY.values()), _w)
+buf("tiny", sum(w for o, w in TINY.values()), F32)
+for _n, _w in (("ysb", 384), ("olb", 384), ("iotap", 256)):
+    buf(_n, _w, F32)
+for _n, _w in (("qi", 1), ("qi2", 1), ("im", 16), ("nmi", 8)):
+    buf(_n, _w, I32)
+for _n, _w in (("lm", 16), ("ends", 1), ("ends2", 1), ("nw16", 16), ("v16", 16), ("d16", 16), ("src16", 8), ("la0", 8)):
+    buf(_n, _w, U16)
+for _t in range(R):
+    buf("g%d" % _t, 1536)
+    buf("trw%d" % _t, 384)
+    buf("pt%d" % _t, 128)
+    buf("alive%d" % _t, 384)
+    buf("bt%d" % _t, 512)
+    buf("sa%d" % _t, 8, U16)
+    buf("la%d" % (_t + 1), 8, U16)
+    buf("qb%d" % _t, 128, Q8)
+    buf("sb%d" % _t, 128, U8)
+for _n, _w in (("u", 128), ("v", 128), ("w", 512), ("e", 512), ("n", 256), ("bit", 128), ("z", 256),
+               ("x0", 256), ("x1", 256), ("x2", 256), ("x3", 256), ("f0", 128), ("f1", 128), ("f2", 128), ("f3", 128)):
+    buf("q" + _n, _w, Q8)
+    buf("s" + _n, _w, U8)
+for _n in range(8):
+    buf("p%d" % _n, 512, F32, "psum")
+
+NDMA = 22
+SEMAPHORES = ["cv", "cs", "cp", "cg", "left"] + ["ra%d" % t for t in range(R)] + ["rb%d" % t for t in range(R)] + ["d%d" % i for i in range(NDMA)]
+
+
+def rank_program(g, core, T, topo):
+    rank = T.rank_of(core)
+    if rank is None:
+        return
+    queues = {"V": g.vector, "S": g.scalar, "P": g.tensor, "G": g, "Y": g.sync}
+    semof = {"V": "cv", "S": "cs", "P": "cp", "G": "cg"}
+    count = {"cv": 0, "cs": 0, "cp": 0, "cg": 0}
+    seen = {q: {} for q in queues}
+    hist, dmas, left, turn = {}, [0], [0], [0, 0]
+
+    def wait(q, needs):
+        for s in sorted(needs):
+            if seen[q].get(s, 0) < needs[s]:
+                queues[q].wait_ge(T.sem[s], needs[s])
+                seen[q][s] = needs[s]
+
+    def need_of(q, reads, writes):
+        needs = {}
+        for refs, wr in ((reads, False), (writes, True)):
+            for name, lo, hi, *ph in refs:
+                psum = SCRATCH[name][0] == "psum"
+                for l, h, w, q2, s, n, *ph2 in hist.get(name, []):
+                    if l < hi and lo < h and (w or wr or (psum and q2 != q)) and not (ph and ph2 and ph != ph2):
+                        needs[s] = max(needs.get(s, 0), n)
+        return needs
+
+    def note(q, reads, writes, s, n):
+        for name, lo, hi, *ph in writes:
+            hist[name] = [r for r in hist.get(name, []) if not (lo <= r[0] and r[1] <= hi and (not ph or list(r[6:]) == ph))] + [(lo, hi, True, q, s, n, *ph)]
+        for name, lo, hi, *ph in reads:
+            hist[name] = [r for r in hist.get(name, []) if r[2] or r[3] != q or not (lo <= r[0] and r[1] <= hi)] + [(lo, hi, False, q, s, n)]
+
+    def emit(q, fn, reads, writes):
+        wait(q, need_of(q, reads, writes))
+        s = semof[q]
+        count[s] += 1
+        fn().then_inc(T.sem[s], 1)
+        note(q, reads, writes, s, count[s])
+
+    def dma(q, o, i, reads, writes):
+        wait(q, need_of(q, reads, writes))
+        s = "d%d" % dmas[0]
+        dmas[0] += 1
+        queues[q].dma_start(o, i).then_inc(T.sem[s], 16)
+        note(q + "d", reads, writes, s, 16)
+
+    def v(name, a=0, b=None, st=None):
+        if name in TINY:
+            o, n = TINY[name]
+            return v("tiny", o + a, o + (n if b is None else b), st)
+        b = SCRATCH[name][1][1] if b is None else b
+        view = T[name][:, a:b] if st is None else T[name][:, a:b:st]
+        return view, [(name, a, b) if st != 4 else (name, a, b, a % 4)]
+
+    def ps(bank, n, a=0):
+        return T["p%d" % bank][:, a:a + n], [("p%d" % bank, 0, 512)]
+
+    def ind(win, lst):
+        return win[0].indirect(lst[0]), win[1] + lst[1]
+
+    def tt(o, a, b, op):
+        emit("V", lambda: g.vector.tensor_tensor(o[0], a[0], b[0], op), a[1] + b[1], o[1])
+
+    def ts(o, a, s1, op0, s2=None, op1=None):
+        r, x = list(a[1]), [s1, s2]
+        for i in (0, 1):
+            if isinstance(x[i], tuple):
+                r += x[i][1]
+                x[i] = x[i][0]
+        if op1 is None:
+            emit("V", lambda: g.vector.tensor_scalar(o[0], a[0], x[0], None, op0), r, o[1])
+        else:
+            emit("V", lambda: g.vector.tensor_scalar(o[0], a[0], x[0], x[1], op0, op1), r, o[1])
+
+    def cp(o, a):
+        emit("V", lambda: g.vector.tensor_copy(o[0], a[0]), a[1], o[1])
+
+    def scan(o, d0, d1, init, op0, op1):
+        emit("V", lambda: g.vector.tensor_tensor_scan(o[0], d0[0], d1[0], init, op0, op1), d0[1] + d1[1], o[1])
+
+    def fill(o, c):
+        emit("V", lambda: g.vector.memset(o[0], c), [], o[1])
+
+    def act(o, a, func, bias=None, scale=1.0, acc=None):
+        r, w, kw = list(a[1]), list(o[1]), {"scale": scale}
+        if bias is not None:
+            kw["bias"] = bias[0]
+            r += bias[1]
+        if acc is not None:
+            kw["accum_out"] = acc[0]
+            w += acc[1]
+        emit("S", lambda: g.scalar.activation(o[0], a[0], func, **kw), r, w)
+
+    def quant(name, src, n, a=0):
+        q, s = v("q" + name, a, a + n), v("s" + name, a, a + n)
+        emit("V", lambda: g.vector.quantize_mx(q[0], s[0], src[0]), src[1], q[1] + s[1])
+
+    def mm(bank, n, l, la, r, ra=0):
+        o = ps(bank, n)
+        lq, ls = v("q" + l, la, la + 128), v("s" + l, la, la + 128)
+        rq, rs = v("q" + r, ra, ra + n), v("s" + r, ra, ra + n)
+        emit("P", lambda: g.tensor.matmul_mx(o[0], lq[0], ls[0], rq[0], rs[0], True, True), lq[1] + ls[1] + rq[1] + rs[1], o[1])
+
+    def iota(o, pattern, base=0, cm=0, small=True):
+        if small:
+            emit("G", lambda: g.iota(o[0], pattern, base, cm, allow_small_or_imprecise_dtypes=True), [], o[1])
+        else:
+            emit("G", lambda: g.iota(o[0], pattern, base, cm), [], o[1])
+
+    def keep_where(o, pattern, op, base, cm):
+        emit("G", lambda: g.affine_select(o[0], o[0], pattern, op, 0.0, base, cm), o[1], o[1])
+
+    dma("Y", T.xin[:], T.x[:], [], v("xin")[1])
+    dma("S", T.uin[:], T.u[:], [], v("uin")[1])
+    dma("Y", T.nmi[:], T.nm[:], [], v("nmi")[1])
+    dma("S", T.hin[:], T.h[:], [], v("hin")[1])
+    dma("Y", T.qw[:, 0:512].bitcast(dt.uint8), T.wc[:, 0:2048], [], v("qw")[1])
+    dma("S", T.sw[:], T.ws[:], [], v("sw")[1])
+    dma("Y", T.vin[:], T.v[:], [], v("vin")[1])
+
+    iota(v("qi"), [[0, 1]], 0, 1, small=False)
+    iota(v("o16"), [[1, 16]])
+    fill(v("blk"), 1.0)
+    fill(v("tmpl", 0, 240), 1.0)
+    fill(v("tmpl", 256, 257), 2048.0)
+    keep_where(v("blk"), [[-16, 8], [0, 16]], A.is_ge, 0, 1)
+    keep_where(v("blk"), [[16, 8], [0, 16]], A.is_ge, 15, -1)
+    iota(v("r16"), [[0, 16], [1, 16]])
+    emit("V", lambda: g.vector.tensor_scalar(T.qi2[:], T.qi[:], 15, None, A.bitwise_and), v("qi")[1], v("qi2")[1])
+    cp(v("kap"), v("qi2"))
+    fill(v("inc", 0, 1), 2048.0)
+    ts(v("own1"), v("o16"), v("kap"), A.is_lt)
+    ts(v("own2"), v("o16"), v("kap"), A.is_equal, -256.0, A.mult)
+    ts(v("pe16"), v("o16"), v("kap"), A.is_lt, 1.0, A.add)
+    tt(v("tmpl", 240, 256), v("own1"), v("own2"), A.add)
+    scan(v("pwv"), v("pe16"), v("pe16"), 1.0, A.mult, A.max)
+    fill(v("ntile"), 0.0)
+    for m in range(15, -1, -1):
+        n = 16 * m + 15 + (m < 15)
+        act(v("inc", off1(m) + 1, off1(m) + 1 + n), v("tmpl", 241 - 16 * m, 241 - 16 * m + n), F.Copy)
+    ts(v("pw"), v("kap"), 6.5, A.is_lt, v("pwv", 15, 16), A.mult)
+    fill(v("bits"), 0.0)
+    iota(v("im"), [[1, 16]], 0, 0, small=False)
+    iota(v("base0"), [[16, 16]], -257)
+    iota(v("plc"), [[1, 128]], 1)
+    iota(v("plcr"), [[-1, 128]], 128)
+    fill(v("idn"), HALF)
+    keep_where(v("idn"), [[-1, 128]], A.is_equal, 0, 1)
+    iota(v("ctile"), [[0, 2048]])
+    iota(v("iota"), [[1, 384]], -128)
+    iota(v("iotap"), [[1, 256]])
+    iota(v("keep2", 256, S2), [[0, S2 - 256]], 1)
+    iota(v("sc2", S2, S2 + 16), [[512, 16]])
+    iota(v("zeros"), [[0, 256]])
+    iota(v("alive0"), [[0, 384]], 1)
+    iota(v("ones"), [[0, 384]], 1)
+    iota(v("thr0"), [[16, 8]])
+    iota(v("c2"), [[32, 8]], 272)
+    iota(v("c2l"), [[-32, 8]], 496)
+    for i in range(1, R):
+        iota(v("alive%d" % i), [[0, 384]], 1)
+    ts(v("ntile", 0, 512, 4), v("blk"), v("pw"), A.mult)
+    ts(v("ntile", 513, 1024, 4), v("blk"), v("pw"), A.mult)
+    quant("n", v("ntile"), 256)
+    quant("u", v("uin"), 128)
+    ts(v("diag"), v("r16"), v("kap"), A.is_equal)
+    for hf in (0, 1):
+        quant("x0", v("xin", 512 * hf, 512 * hf + 512), 128, 128 * hf)
+        mm(hf, 128, "u", 0, "x0", 128 * hf)
+    ts(v("keep"), v("r16"), 0.0, A.not_equal)
+
+    def x_of(t, b, a=0, e=256):
+        return v("gx" if t == 0 else "g%d" % (t - 1), 384 * b + 128 + a, 384 * b + 128 + e)
+
+    def front_of(t, b):
+        return v("g%d" % t, 384 * b, 384 * b + 128)
+
+    def decode_x(t, planes):
+        for b in planes:
+            mm(4 + b, 256, "e", 128 * b, "x%d" % t)
+
+    def copy_x(t, planes, q="S"):
+        for b in planes:
+            if q == "S":
+                act(x_of(t, b), ps(4 + b, 256), F.Copy)
+            else:
+                cp(x_of(t, b), ps(4 + b, 256))
+
+    def decode_f(t):
+        for b in range(4):
+            mm(b, 128, "e", 128 * b, "f%d" % t)
+            act(front_of(t, b), ps(b, 128), F.Copy)
+
+    def names_in(t):
+        p = "plcr" if t else "plc"
+        emit("V", lambda: g.vector.tensor_copy(T["pt%d" % t][:, 0:128].indirect(T["la%d" % t][:, 0:8]), T[p][:]),
+             v(p)[1] + v("la%d" % t)[1], v("pt%d" % t)[1])
+
+    def names_row(t):
+        act(v("trw%d" % t, 0, 128), ind(v("iotap", 0, 128), v("la%d" % t)), F.Copy)
+
+    nxt = T.cores[(rank + 1) % len(T.cores)]
+    rid, pid = topo.addr(nxt, core)
+    eng = topo.engines(core, nxt)[:8]
+    mask = sum(1 << e for e in eng)
+
+    def send(dst, src, rsem, reads):
+        wait("G", need_of("G", reads, []))
+        g.remote_dma(dst, src, T.sem[rsem], T.sem.left, pid, rid, mask)
+        left[0] += len(eng)
+
+    def send_names(t):
+        send(T["la%d" % (t + 1)][:], T["sa%d" % t][:], "ra%d" % t, v("sa%d" % t)[1])
+        hist["la%d" % (t + 1)] = [(0, 8, True, "R", "ra%d" % t, len(eng))]
+
+    def border_send(t):
+        quant("b%d" % t, v("bt%d" % t), 128)
+        send(T["qf%d" % (t + 1)][:, 0:128].bitcast(dt.uint8), T["qb%d" % t][:, 0:128].bitcast(dt.uint8), "rb%d" % t, v("qb%d" % t)[1])
+        send(T["sf%d" % (t + 1)][:], T["sb%d" % t][:], "rb%d" % t, v("sb%d" % t)[1])
+        for n in ("qf%d", "sf%d"):
+            hist[n % (t + 1)] = [(0, 128, True, "R", "rb%d" % t, 2 * len(eng))]
+
+    def border_alive(t):
+        emit("V", lambda: g.vector.tensor_copy(T["alive%d" % t][:, 0:384].indirect(T.v16[:, 0:16]), T.zeros[:]),
+             v("zeros")[1] + v("v16")[1] + v("alive%d" % t)[1], v("alive%d" % t)[1])
+        scan(v("arow"), v("ones"), v("alive%d" % t), 0.0, A.mult, A.add)
+
+    def junk(n):
+        turn[0] = (turn[0] + 1) % 4
+        return v("junk", 384 * turn[0], 384 * turn[0] + n)
+
+    def border_count(t, ms, q="S"):
+        last = t == R - 1
+        thr = "thrl" if last else "thr"
+        for m in ms:
+            a = 112 - 16 * m if last else 16 * m
+            if q == "S":
+                act(junk(272), v("arow", a, a + 272), F.Sign, bias=v(thr, m, m + 1), scale=-1.0, acc=v("accb", m, m + 1))
+            else:
+                turn[1] = (turn[1] + 1) % 3
+                o = v("ltb", 272 * turn[1], 272 * turn[1] + 272)
+                ts(o, v("arow", a, a + 272), v(thr, m, m + 1), A.is_lt, 2.0, A.mult)
+                scan(v("cs", 272 * m, 272 * m + 272), v("ones", 0, 272), o, -272.0, A.mult, A.add)
+
+    def border_columns(t):
+        n, c2 = (NLAST, "c2l") if t == R - 1 else (NMID, "c2")
+        yield tt(v("sb_", n, 8), v("cs", 272 * n + 271, 2176, 272), v(c2, n, 8), A.add)
+        yield tt(v("sb_", 0, n), v("accb", 0, n), v(c2, 0, n), A.add)
+        if t == 0:
+            yield ts(v("sa_"), v("sb_"), 255.5, A.is_ge, 0.5, A.mult)
+            yield ts(v("sc_"), v("sb_"), -0.5, A.mult, 127.0, A.add)
+            yield tt(v("sa_"), v("sa_"), v("sb_"), A.mult)
+            yield tt(v("sf_"), v("sa_"), v("sc_"), A.max)
+            yield cp(v("src16"), v("sf_"))
+        else:
+            yield ts(v("src16"), v("sb_"), 0.5, A.mult)
+
+    def border_names(t):
+        yield tt(v("mn"), ind(v("trw%d" % t), v("src16")), v("diag", 0, 128), A.mult)
+        yield scan(v("mh"), v("keep", 0, 128), v("mn"), 0.0, A.mult, A.add)
+        yield cp(v("sa%d" % t), v("mh", 15, 128, 16))
+        send_names(t)
+
+    def border_list(t):
+        yield from border_columns(t)
+        yield from border_names(t)
+
+    def border_gather(t, b, q):
+        o, i = v("bt%d" % t, b, 512, 4), ind(v("g%d" % t, 384 * b, 384 * b + 384), v("src16"))
+        if q == "S":
+            act(o, i, F.Copy, scale=2.0)
+        else:
+            ts(o, i, 2.0, A.mult)
+
+    for t in range(R):
+        tr = "trw%d" % t
+        ts(v("bits", 0, 512, 4), ps(0, 128), 0.0, A.is_lt)
+        ts(v("bits", 1, 512, 4), ps(1, 128), 0.0, A.is_lt)
+        quant("bit", v("bits"), 128)
+        mm(2, 128, "n", 0, "bit")
+        mm(3, 128, "n", 128, "bit")
+        if t > 0:
+            decode_x(t, range(4))
+            border_count(t - 1, range(NMID, 8), "V")
+        else:
+            cp(v("la0"), v("nmi"))
+            names_in(0)
+            cp(v("lm"), v("im"))
+        for hf in (0, 1):
+            a, e = 128 * hf, 128 * hf + 128
+            tt(v("hm", a, e), ps(2 + hf, 128), v("diag", a, e), A.mult)
+            act(v(tr, 128 + a, 128 + e), ps(2 + hf, 128), F.Copy)
+        if t > 0:
+            border_count(t - 1, range(NEARLY, NMID))
+        scan(v("hold"), v("keep"), v("hm"), 0.0, A.mult, A.add)
+        if t == 0:
+            for b in range(4):
+                act(v("ctile", 512 * b + b, 512 * b + 512, 4), v("idn"), F.Copy)
+            ts(v("base"), v("base0"), v("kap"), A.add)
+            ts(v("k1"), v("kap"), 1.5, A.add)
+            ts(v("e1"), v("kap"), 16.0 * MS + 16.0, A.mult, 255.0 - 16.0 * MS, A.add)
+            ts(v("e3"), v("kap"), -16.0 * MS, A.mult, 255.0 + 16.0 * MS * MS, A.add)
+            ts(v("e2"), v("kap"), float(S2), A.add)
+            ts(v("sel1"), v("kap"), 0.5, A.is_ge)
+            tt(v("k2"), v("k1"), v("k1"), A.mult)
+            tt(v("pe"), v("e1"), v("e3"), A.min)
+            ts(v("sel2"), v("kap"), MS - 0.5, A.is_lt, v("sel1"), A.mult)
+            ts(v("ends"), v("k2"), 8.0, A.mult, -3.0, A.add)
+            ts(v("pr"), v("pe"), v("e2"), A.subtract, v("sel2"), A.mult)
+            fill(v("bm64"), -64.0)
+            ts(v("ends2"), v("pr"), v("e2"), A.add)
+        else:
+            copy_x(t, range(4))
+        steps = border_list(t - 1) if t > 0 else iter(())
+        for m in range(16):
+            ts(v("qq", off1(m), off1(m + 1)), v(tr, 128, 144 + 16 * m), v("hold", 16 * m + 15, 16 * m + 16), A.not_equal, 1024.0, A.mult)
+            if m >= LSTEP:
+                next(steps, None)
+        cp(v("nw16"), v("hold", 15, 256, 16))
+        for x in steps:
+            pass
+        if t == 0:
+            quant("f0", v("hin"), 128)
+        else:
+            for b in range(4):
+                border_gather(t - 1, b, "S")
+        scan(v("sc"), v("inc"), v("qq"), 0.0, A.add, A.min)
+        if t > 0:
+            border_send(t - 1)
+        else:
+            quant("e", v("ctile"), 512)
+            decode_x(0, range(4))
+            copy_x(0, range(4))
+        ts(v("nh"), ind(v("sc"), v("ends")), -0.5, A.is_ge, 1024.0, A.mult)
+        tt(v("x1"), ind(v("sc"), v("ends")), v("base"), A.subtract)
+        if t > 0:
+            names_in(t)
+        names_row(t)
+        tt(v("pl"), ind(v("pt%d" % t), v("nw16")), v("diag"), A.mult)
+        tt(v("w1"), v("x1"), v("nh"), A.add)
+        scan(v("plh"), v("keep"), v("pl"), 0.0, A.mult, A.add)
+        tt(v("w"), v("w1"), v("plh", 15, 256, 16), A.min)
+        ts(v("v16"), v("w"), -1.0, A.mult, 128.0, A.add)
+        act(v("vw"), v("w"), F.Copy, scale=-1.0)
+        act(v("e32", 0, 16), v("w"), F.Identity, bias=v("bm64"), scale=64.0)
+        cp(v("vr"), ind(v("iota"), v("v16")))
+        if t == 0:
+            ts(v("keep2", 0, 256), v("diag"), 63.0, A.mult, 1.0, A.add)
+            fill(v("keep2", 0, 256, 16), 0.0)
+            fill(v("keep2", 256, S2, 16 * MS), 0.0)
+            fill(v("keep2", 272, S2, 16 * MS + 16), 0.0)
+        for m in range(MS, 16):
+            act(junk(16 * m), v("vr", 0, 16 * m), F.Sign, bias=v("vw", m, m + 1), scale=-1.0, acc=v("acc", m, m + 1))
+        act(v("e32", 16 + MS, 32), v("acc", MS, 16), F.Copy, scale=32.0)
+
+        def shorter(a, b):
+            for m in range(a, b):
+                ts(v("lt", off2(m), off2(m) + 16 * m), v("vr", 0, 16 * m), v("vw", m, m + 1), A.is_lt, 64.0, A.mult)
+
+        tt(v("lt", 0, 256), ind(v("vw"), v("lm")), v("vr"), A.is_gt)
+        shorter(1, 4)
+        scan(v("sc2", 0, 256), v("keep2", 0, 256), v("lt", 0, 256), 0.0, A.mult, A.add)
+        shorter(4, MS)
+        tt(v("dd"), v("sc2", 15, 256, 16), v("e32", 0, 16), A.add)
+        scan(v("sc2", 256, S2), v("keep2", 256, S2), v("lt", 256, S2), 0.0, A.mult, A.add)
+        tt(v("dd", MS, 16), v("dd", MS, 16), v("e32", 16 + MS, 32), A.add)
+        tt(v("d"), ind(v("sc2"), v("ends2")), v("dd"), A.add)
+        if t == 0:
+            ts(v("d16"), v("d"), 1.0 / 64, A.mult)
+        else:
+            ts(v("d16"), v("d"), -1.0 / 64, A.mult, 127.0, A.add)
+        decode_f(t)
+        for hf in (0, 1):
+            a, e = 128 * hf, 128 * hf + 128
+            for b in range(4):
+                tt(v("zt", 4 * a + b, 4 * e, 4), ind(front_of(t, b), v("d16", 8 * hf, 8 * hf + 8)), x_of(t, b, a, e), A.add)
+            quant("z", v("zt", 4 * a, 4 * e), 128, a)
+            for b in range(4):
+                mm(4 * hf + b, 128, "w", 128 * b, "z", a)
+        if t == 0:
+            ts(v("thr"), v("thr0"), v("kap"), A.add, 0.5, A.add)
+        border_alive(t)
+        if t == 0:
+            ts(v("thrl"), v("thr"), -1.0, A.mult, 128.0, A.add)
+            fill(v("b127"), 127.0)
+        for hf in (0, 1):
+            a, e = 128 * hf, 128 * hf + 128
+            for b in range(4):
+                if hf == 1 and b >= YV:
+                    ts(v("yt", 4 * a + b, 4 * e, 4), ps(4 * hf + b, 128), 0.03125, A.mult)
+                else:
+                    act(v("yt", 4 * a + b, 4 * e, 4), ps(4 * hf + b, 128), F.Copy, scale=0.03125)
+            quant("x%d" % (t + 1), v("yt", 4 * a, 4 * e), 128, a)
+            if t < R - 1:
+                mm(hf, 128, "u", 0, "x%d" % (t + 1), a)
+        if t < R - 1:
+            border_count(t, range(NEARLY))
+
+    decode_x(R, range(4))
+    border_count(R - 1, range(NLAST))
+    border_count(R - 1, range(NLAST, 7), "V")
+    copy_x(R, (0, 1, 3))
+    copy_x(R, (2,), "V")
+    border_count(R - 1, (7,), "V")
+    for x in border_columns(R - 1):
+        pass
+    for b in (0, 1):
+        border_gather(R - 1, b, "S")
+    for b in (2, 3):
+        border_gather(R - 1, b, "V")
+    border_send(R - 1)
+    for x in border_names(R - 1):
+        pass
+    quant("v", v("vin"), 128)
+    mm(1, 256, "v", 0, "x3")
+    act(v("ysb", 0, 256), ps(1, 256), F.Copy)
+    act(v("olb", 0, 256), ind(v("iotap"), v("d16")), F.Identity, bias=v("b127"), scale=-1.0)
+
+    def stores(a, n, q, s):
+        dma("Y", T.oc[:, 4 * a:4 * (a + n)], T[q][:, 0:n].bitcast(dt.uint8), v(q)[1], [])
+        for k in range(4):
+            dma("Y" if k % 2 else "S", T.osc[4 * k:4 * k + 4, a:a + n], T[s][32 * k:32 * k + 4, 0:n], v(s)[1], [])
+
+    dma("S", T.y[:, 0:256], T.ysb[:, 0:256], v("ysb", 0, 256)[1], [])
+    stores(0, 256, "qx3", "sx3")
+    mm(2, 128, "v", 0, "f3")
+    cp(v("ysb", 256, 384), ps(2, 128))
+    stores(256, 128, "qf3", "sf3")
+    dma("Y", T.y[:, 256:384], T.ysb[:, 256:384], v("ysb", 256, 384)[1], [])
+    act(v("olb", 256, 384), ind(v("iotap"), v("la3")), F.Copy)
+    dma("S", T.ol[:, :], T.olb[0:128:16, :], v("olb")[1], [])
+
+    for s in ("cv", "cs", "cp", "cg"):
+        g.wait_ge(T.sem[s], count[s])
+    for i in range(dmas[0]):
+        g.wait_ge(T.sem["d%d" % i], 16)
+    for i in range(R):
+        g.wait_ge(T.sem["ra%d" % i], len(eng))
+        g.wait_ge(T.sem["rb%d" % i], 2 * len(eng))
+    g.wait_ge(T.sem.left, left[0])

@@ -1,24 +1,19 @@
-from concourse.mybir import dt, AluOpType as A, ActivationFunctionType as F, AxisListType
+from concourse.mybir import dt, AluOpType as A, ActivationFunctionType as F
 
 C, K, R = 256, 128, 3
-MS = 11
-NMID = 7
-NEARLY = 5
-NLAST = 4
-LSTEP = 9
-YV = 3
-HALF = 0.5
+NS = 0
+O1 = -128.0
 
 
 def off1(m):
-    return 8 * m * (m + 1)
+    return 129 * m - 8 * m * (m - 1)
 
 
 def off2(m):
-    return 256 + 16 * MS * (m - 1) if 2 * m <= MS else 256 + 16 * MS * (MS - m - 1) + 16 * (MS - m)
+    return 8 * m * (m + 1)
 
 
-S2 = 256 + 8 * MS * (MS - 1)
+S1, S2 = off1(8), off2(8)
 BF, F32, I32, U16, U8, Q8 = "bfloat16", "float32", "int32", "uint16", "uint8", "float8_e4m3fn_x4"
 SCRATCH, TINY = {}, {}
 
@@ -27,36 +22,31 @@ def buf(name, n, d=BF, where="sbuf"):
     SCRATCH[name] = (where, [128, n], d)
 
 
-for _n, _w in (("xin", 1024), ("hin", 512), ("uin", 512), ("vin", 512), ("bits", 512), ("ctile", 2048), ("ntile", 1024),
-               ("zt", 1024), ("yt", 1024), ("blk", 128), ("idn", 128), ("o16", 16), ("pe16", 16), ("r16", 256), ("diag", 256),
-               ("keep", 256), ("keep2", S2), ("tmpl", 272), ("own1", 16), ("own2", 16), ("inc", 2176), ("iota", 384), ("plc", 128),
-               ("plcr", 128), ("zeros", 256), ("ones", 384), ("hm", 256), ("hold", 256), ("qq", 2176), ("sc", 2176), ("pl", 256),
-               ("plh", 256), ("vr", 256), ("vw", 16), ("lt", S2), ("sc2", S2 + 16), ("junk", 1536), ("ltb", 816), ("cs", 2176),
-               ("mn", 128), ("mh", 128), ("arow", 384), ("gx", 1536)):
+for _n, _w in (("xin", 1024), ("hin", 512), ("uin", 512), ("vin", 512), ("bits0", 512), ("bits1", 512), ("ctile", 516), ("ntile", 512),
+               ("zt", 1024), ("yt", 1024), ("blk", 128), ("o16", 18), ("pe16", 16), ("r16", 128), ("st1", 128), ("st2", 128), ("st3", 128),
+               ("sta", 128), ("tm1", 130), ("tm2", 128), ("inc", S1), ("keep", S2), ("iota", 256), ("plc", 128), ("nms", 128), ("row", 288),
+               ("hold", 256), ("qq0", S1), ("qq1", S1), ("sc0", S1), ("sc1", S1), ("w0", 256), ("w1", 256), ("r1", 128), ("vh", 384),
+               ("lh0", 128), ("lt0", S2), ("lt1", S2), ("cs0", S2), ("cs1", S2), ("junk", 512), ("srow", 128), ("gx", 1536), ("n2b", 1)):
     buf(_n, _w)
-for _n, _w in (("kap", 1), ("pw", 1), ("k1", 1), ("k2", 1), ("e1", 1), ("e2", 1), ("e3", 1), ("pe", 1), ("sel1", 1), ("sel2", 1), ("pr", 1),
-               ("base", 16), ("base0", 16), ("thr", 8), ("pwv", 16),
-               ("thr0", 8), ("thrl", 8), ("x1", 16), ("nh", 16), ("w1", 16), ("w", 16), ("acc", 16), ("e32", 32), ("dd", 16), ("d", 16), ("accb", 8),
-               ("sa_", 8), ("sb_", 8), ("sc_", 8), ("sf_", 8), ("c2", 8), ("c2l", 8), ("b127", 1), ("bm64", 1)):
+for _n, _w in (("nw0", 16), ("nw1", 16), ("kap", 1), ("pw", 1), ("k1", 1), ("k8", 1), ("a1", 1), ("a2", 1), ("n1", 1), ("n2", 1), ("n3", 1), ("nb", 1),
+               ("cs", 1), ("pwv", 16), ("nb0", 8), ("nb1", 8), ("x0", 16), ("x1", 16), ("y0", 16), ("y1", 16), ("lw0", 8), ("lw1", 8),
+               ("acc0", 8), ("acc1", 8)):
     TINY[_n] = (sum(w for o, w in TINY.values()), _w)
 buf("tiny", sum(w for o, w in TINY.values()), F32)
-for _n, _w in (("ysb", 384), ("olb", 384), ("iotap", 256)):
+for _n, _w in (("ysb", 384), ("olb", 384), ("lh1", 128), ("sh", 128)):
     buf(_n, _w, F32)
-for _n, _w in (("qi", 1), ("qi2", 1), ("im", 16), ("nmi", 8)):
+for _n, _w in (("qi", 1), ("qi2", 1), ("nmi", 8)):
     buf(_n, _w, I32)
-for _n, _w in (("lm", 16), ("ends", 1), ("ends2", 1), ("nw16", 16), ("v16", 16), ("d16", 16), ("src16", 8), ("la0", 8)):
+for _n, _w in (("ends1", 1), ("ends2", 1), ("nw16", 16), ("off16", 16), ("d16", 16), ("src16", 8), ("la0", 8), ("lm", 8)):
     buf(_n, _w, U16)
 for _t in range(R):
     buf("g%d" % _t, 1536)
-    buf("trw%d" % _t, 384)
-    buf("pt%d" % _t, 128)
-    buf("alive%d" % _t, 384)
     buf("bt%d" % _t, 512)
     buf("sa%d" % _t, 8, U16)
     buf("la%d" % (_t + 1), 8, U16)
     buf("qb%d" % _t, 128, Q8)
     buf("sb%d" % _t, 128, U8)
-for _n, _w in (("u", 128), ("v", 128), ("w", 512), ("e", 512), ("n", 256), ("bit", 128), ("z", 256),
+for _n, _w in (("u", 128), ("v", 128), ("w", 512), ("e", 512), ("n", 128), ("bit0", 128), ("bit1", 128), ("z", 256),
                ("x0", 256), ("x1", 256), ("x2", 256), ("x3", 256), ("f0", 128), ("f1", 128), ("f2", 128), ("f3", 128)):
     buf("q" + _n, _w, Q8)
     buf("s" + _n, _w, U8)
@@ -75,7 +65,7 @@ def rank_program(g, core, T, topo):
     semof = {"V": "cv", "S": "cs", "P": "cp", "G": "cg"}
     count = {"cv": 0, "cs": 0, "cp": 0, "cg": 0}
     seen = {q: {} for q in queues}
-    hist, dmas, left, turn = {}, [0], [0], [0, 0]
+    hist, dmas, left, turn = {}, [0], [0], [0]
 
     def wait(q, needs):
         for s in sorted(needs):
@@ -121,8 +111,8 @@ def rank_program(g, core, T, topo):
         view = T[name][:, a:b] if st is None else T[name][:, a:b:st]
         return view, [(name, a, b) if st != 4 else (name, a, b, a % 4)]
 
-    def ps(bank, n, a=0):
-        return T["p%d" % bank][:, a:a + n], [("p%d" % bank, 0, 512)]
+    def ps(bank, n):
+        return T["p%d" % bank][:, 0:n], [("p%d" % bank, 0, 512)]
 
     def ind(win, lst):
         return win[0].indirect(lst[0]), win[1] + lst[1]
@@ -144,6 +134,9 @@ def rank_program(g, core, T, topo):
     def cp(o, a):
         emit("V", lambda: g.vector.tensor_copy(o[0], a[0]), a[1], o[1])
 
+    def scatter(win, lst, a):
+        emit("V", lambda: g.vector.tensor_copy(win[0].indirect(lst[0]), a[0]), a[1] + lst[1], win[1])
+
     def scan(o, d0, d1, init, op0, op1):
         emit("V", lambda: g.vector.tensor_tensor_scan(o[0], d0[0], d1[0], init, op0, op1), d0[1] + d1[1], o[1])
 
@@ -152,9 +145,11 @@ def rank_program(g, core, T, topo):
 
     def act(o, a, func, bias=None, scale=1.0, acc=None):
         r, w, kw = list(a[1]), list(o[1]), {"scale": scale}
-        if bias is not None:
+        if isinstance(bias, tuple):
             kw["bias"] = bias[0]
             r += bias[1]
+        elif bias is not None:
+            kw["bias"] = bias
         if acc is not None:
             kw["accum_out"] = acc[0]
             w += acc[1]
@@ -179,94 +174,9 @@ def rank_program(g, core, T, topo):
     def keep_where(o, pattern, op, base, cm):
         emit("G", lambda: g.affine_select(o[0], o[0], pattern, op, 0.0, base, cm), o[1], o[1])
 
-    dma("Y", T.xin[:], T.x[:], [], v("xin")[1])
-    dma("S", T.uin[:], T.u[:], [], v("uin")[1])
-    dma("Y", T.nmi[:], T.nm[:], [], v("nmi")[1])
-    dma("S", T.hin[:], T.h[:], [], v("hin")[1])
-    dma("Y", T.qw[:, 0:512].bitcast(dt.uint8), T.wc[:, 0:2048], [], v("qw")[1])
-    dma("S", T.sw[:], T.ws[:], [], v("sw")[1])
-    dma("Y", T.vin[:], T.v[:], [], v("vin")[1])
-
-    iota(v("qi"), [[0, 1]], 0, 1, small=False)
-    iota(v("o16"), [[1, 16]])
-    fill(v("blk"), 1.0)
-    fill(v("tmpl", 0, 240), 1.0)
-    fill(v("tmpl", 256, 257), 2048.0)
-    keep_where(v("blk"), [[-16, 8], [0, 16]], A.is_ge, 0, 1)
-    keep_where(v("blk"), [[16, 8], [0, 16]], A.is_ge, 15, -1)
-    iota(v("r16"), [[0, 16], [1, 16]])
-    emit("V", lambda: g.vector.tensor_scalar(T.qi2[:], T.qi[:], 15, None, A.bitwise_and), v("qi")[1], v("qi2")[1])
-    cp(v("kap"), v("qi2"))
-    fill(v("inc", 0, 1), 2048.0)
-    ts(v("own1"), v("o16"), v("kap"), A.is_lt)
-    ts(v("own2"), v("o16"), v("kap"), A.is_equal, -256.0, A.mult)
-    ts(v("pe16"), v("o16"), v("kap"), A.is_lt, 1.0, A.add)
-    tt(v("tmpl", 240, 256), v("own1"), v("own2"), A.add)
-    scan(v("pwv"), v("pe16"), v("pe16"), 1.0, A.mult, A.max)
-    fill(v("ntile"), 0.0)
-    for m in range(15, -1, -1):
-        n = 16 * m + 15 + (m < 15)
-        act(v("inc", off1(m) + 1, off1(m) + 1 + n), v("tmpl", 241 - 16 * m, 241 - 16 * m + n), F.Copy)
-    ts(v("pw"), v("kap"), 6.5, A.is_lt, v("pwv", 15, 16), A.mult)
-    fill(v("bits"), 0.0)
-    iota(v("im"), [[1, 16]], 0, 0, small=False)
-    iota(v("base0"), [[16, 16]], -257)
-    iota(v("plc"), [[1, 128]], 1)
-    iota(v("plcr"), [[-1, 128]], 128)
-    fill(v("idn"), HALF)
-    keep_where(v("idn"), [[-1, 128]], A.is_equal, 0, 1)
-    iota(v("ctile"), [[0, 2048]])
-    iota(v("iota"), [[1, 384]], -128)
-    iota(v("iotap"), [[1, 256]])
-    iota(v("keep2", 256, S2), [[0, S2 - 256]], 1)
-    iota(v("sc2", S2, S2 + 16), [[512, 16]])
-    iota(v("zeros"), [[0, 256]])
-    iota(v("alive0"), [[0, 384]], 1)
-    iota(v("ones"), [[0, 384]], 1)
-    iota(v("thr0"), [[16, 8]])
-    iota(v("c2"), [[32, 8]], 272)
-    iota(v("c2l"), [[-32, 8]], 496)
-    for i in range(1, R):
-        iota(v("alive%d" % i), [[0, 384]], 1)
-    ts(v("ntile", 0, 512, 4), v("blk"), v("pw"), A.mult)
-    ts(v("ntile", 513, 1024, 4), v("blk"), v("pw"), A.mult)
-    quant("n", v("ntile"), 256)
-    quant("u", v("uin"), 128)
-    ts(v("diag"), v("r16"), v("kap"), A.is_equal)
-    for hf in (0, 1):
-        quant("x0", v("xin", 512 * hf, 512 * hf + 512), 128, 128 * hf)
-        mm(hf, 128, "u", 0, "x0", 128 * hf)
-    ts(v("keep"), v("r16"), 0.0, A.not_equal)
-
-    def x_of(t, b, a=0, e=256):
-        return v("gx" if t == 0 else "g%d" % (t - 1), 384 * b + 128 + a, 384 * b + 128 + e)
-
-    def front_of(t, b):
-        return v("g%d" % t, 384 * b, 384 * b + 128)
-
-    def decode_x(t, planes):
-        for b in planes:
-            mm(4 + b, 256, "e", 128 * b, "x%d" % t)
-
-    def copy_x(t, planes, q="S"):
-        for b in planes:
-            if q == "S":
-                act(x_of(t, b), ps(4 + b, 256), F.Copy)
-            else:
-                cp(x_of(t, b), ps(4 + b, 256))
-
-    def decode_f(t):
-        for b in range(4):
-            mm(b, 128, "e", 128 * b, "f%d" % t)
-            act(front_of(t, b), ps(b, 128), F.Copy)
-
-    def names_in(t):
-        p = "plcr" if t else "plc"
-        emit("V", lambda: g.vector.tensor_copy(T["pt%d" % t][:, 0:128].indirect(T["la%d" % t][:, 0:8]), T[p][:]),
-             v(p)[1] + v("la%d" % t)[1], v("pt%d" % t)[1])
-
-    def names_row(t):
-        act(v("trw%d" % t, 0, 128), ind(v("iotap", 0, 128), v("la%d" % t)), F.Copy)
+    def junk():
+        turn[0] = (turn[0] + 1) % 4
+        return v("junk", 128 * turn[0], 128 * turn[0] + 128)
 
     nxt = T.cores[(rank + 1) % len(T.cores)]
     rid, pid = topo.addr(nxt, core)
@@ -278,212 +188,345 @@ def rank_program(g, core, T, topo):
         g.remote_dma(dst, src, T.sem[rsem], T.sem.left, pid, rid, mask)
         left[0] += len(eng)
 
-    def send_names(t):
+    def x_of(t, b, h):
+        return v("gx" if t == 0 else "g%d" % (t - 1), 384 * b + 128 + 128 * h, 384 * b + 256 + 128 * h)
+
+    def front_of(t, b):
+        return v("g%d" % t, 384 * b, 384 * b + 128)
+
+    def scores(t, h):
+        mm(4 * h, 128, "u", 0, "x%d" % t, 128 * h)
+
+    def signs(h):
+        act(v("bits%d" % h, 0, 512, 4), ps(4 * h, 128), F.Sign, bias=2.0 ** -100)
+
+    def names(h):
+        quant("bit%d" % h, v("bits%d" % h), 128)
+        mm(4 * h + 1, 128, "n", 0, "bit%d" % h)
+
+    def name_row(h):
+        act(v("row", 144 * h, 144 * h + 128), ps(4 * h + 1, 128), F.Identity, bias=63.5)
+
+    def wrap(h):
+        scan(v("hold", 128 * h, 128 * h + 128), v("st1"), v("row", 144 * h, 144 * h + 128), 0.0, A.add, A.min)
+
+    def wrapped(h):
+        held = v("hold", 128 * h + 15, 128 * h + 128, 16)
+        ts(v("nw%d" % h, 0, 8), held, v("n1"), A.add)
+        ts(v("nw16", 8 * h, 8 * h + 8), held, v("n1"), A.add)
+        if NS:
+            act(v("nb%d" % h), held, F.Identity, bias=v("nb"), scale=-1024.0)
+
+    def compare(h, q):
+        for m in (range(8 - NS) if q == "V" else range(8 - NS, 8)):
+            o, i = v("qq%d" % h, off1(m), off1(m + 1)), v("row", 144 * h + 16 * m, 144 * h + 129)
+            if q == "V":
+                ts(o, i, v("nw%d" % h, m, m + 1), A.not_equal, 1024.0, A.mult)
+            else:
+                act(o, i, F.Abs, bias=v("nb%d" % h, m, m + 1), scale=1024.0)
+
+    def next_use(h):
+        scan(v("sc%d" % h), v("inc"), v("qq%d" % h), 0.0, A.add, A.min)
+
+    def places(h):
+        yield tt(v("x%d" % h), ind(v("sc%d" % h), v("ends1")), v("nw%d" % h), A.min)
+        yield ts(v("off16", 8 * h, 8 * h + 8), v("x%d" % h, 0, 8), 128.0, A.add)
+
+    def table(t, h):
+        act(v("r1") if h else v("w0", 128, 256), ind(v("iota", 0, 128), v("lm" if h else "la%d" % t)), F.Copy)
+
+    def look_up(h):
+        act(v("w%d" % h, 0, 128), ind(v("r1") if h else v("w0", 128, 256), v("nw16", 8 * h, 8 * h + 8)), F.Copy)
+
+    def hand_on():
+        act(v("w1", 128, 256), v("w0", 128, 256), F.Identity, bias=-8192.0)
+
+    def latest(h):
+        scatter(v("w%d" % h), v("off16", 8 * h, 8 * h + 8), v("iota", 128, 256))
+
+    def wrap_latest(h):
+        scan(v("vh", 128 * h, 128 * h + 128), v("st2"), v("w%d" % h, 0, 128), 0.0, A.add, A.min)
+
+    def counts(h):
+        for m in range(7, -1, -1):
+            c = 128 * h + 16 * m + 15
+            ts(v("lt%d" % h, off2(m), off2(m + 1)), v("w%d" % h, 0, 16 * m + 16), v("n2b"), A.subtract, v("vh", c, c + 1), A.is_lt)
+
+    def count_sums(h):
+        scan(v("cs%d" % h), v("keep"), v("lt%d" % h), 0.0, A.mult, A.add)
+
+    def distance(h):
+        yield tt(v("y%d" % h), ind(v("cs%d" % h), v("ends2")), v("vh", 128 * h + 15, 128 * h + 256, 16), A.subtract)
+        yield ts(v("d16", 8 * h, 8 * h + 8), v("y%d" % h, 0, 8), v("n2"), A.subtract, -1.0 / 64, A.mult)
+
+    def decode_f(t):
+        for b in range(4):
+            mm(b, 128, "e", 128 * b, "f%d" % t)
+
+    def copy_f(t):
+        for b in range(4):
+            i = ps(b, 128) if t else (T["p%d" % b][:, 127::-1], ps(b, 128)[1])
+            act(front_of(t, b), i, F.Copy, scale=0.5)
+
+    def mix(t, h):
+        a, e = 128 * h, 128 * h + 128
+        for b in range(4):
+            tt(v("zt", 4 * a + b, 4 * e, 4), ind(front_of(t, b), v("d16", 8 * h, 8 * h + 8)), x_of(t, b, h), A.add)
+
+    def layer(h):
+        quant("z", v("zt", 512 * h, 512 * h + 512), 128, 128 * h)
+        for b in range(4):
+            mm(4 * h + b, 128, "w", 128 * b, "z", 128 * h)
+
+    def copy_y(h, planes=range(4), q="S"):
+        for b in planes:
+            o = v("yt", 512 * h + b, 512 * h + 512, 4)
+            if q == "S":
+                act(o, ps(4 * h + b, 128), F.Copy, scale=0.03125)
+            else:
+                ts(o, ps(4 * h + b, 128), 0.03125, A.mult)
+
+    def new_x(t, h):
+        quant("x%d" % t, v("yt", 512 * h, 512 * h + 512), 128, 128 * h)
+
+    def xbank(h, b):
+        return ((2, 3, 0, 1), (6, 7, 4, 2))[h][b]
+
+    def decode_x(t, h, planes):
+        for b in planes:
+            mm(xbank(h, b), 128, "e", 128 * b, "x%d" % t, 128 * h)
+
+    def copy_x(t, h, planes, q="S"):
+        for b in planes:
+            if q == "S":
+                act(x_of(t, b, h), ps(xbank(h, b), 128), F.Copy, scale=0.5)
+            else:
+                ts(x_of(t, b, h), ps(xbank(h, b), 128), 0.5, A.mult)
+
+    def last_uses(h):
+        scan(v("lh%d" % h), v("st3" if h else "st2"), v("w%d" % h, 128, 256), 0.0, A.add, A.min)
+
+    def ranks(h):
+        act(v("lw%d" % h), v("lh%d" % h, 15, 128, 16), F.Identity, bias=v("n3" if h else "n2"))
+        for m in range(8):
+            act(junk(), v("w%d" % h, 128, 256), F.Sign, bias=v("lw%d" % h, m, m + 1), scale=-1.0, acc=v("acc%d" % h, m, m + 1))
+
+    def rank_list(t, h):
+        ts(v("sa%d" % t if h else "lm"), v("acc%d" % h), 0.5 if t < R - 1 or not h else -0.5, A.mult, 63.5, A.add)
+
+    def send_ranks(t):
         send(T["la%d" % (t + 1)][:], T["sa%d" % t][:], "ra%d" % t, v("sa%d" % t)[1])
         hist["la%d" % (t + 1)] = [(0, 8, True, "R", "ra%d" % t, len(eng))]
 
-    def border_send(t):
+    def sources(t):
+        yield scatter(v("srow"), v("sa%d" % t), v("w1", 128, 256))
+        yield scan(v("sh"), v("st3"), v("srow"), 0.0, A.add, A.min)
+        yield ts(v("src16"), v("sh", 15, 128, 16), v("cs"), A.add, 1.0 / 64, A.mult)
+
+    def border(t, planes, q="S"):
+        for b in planes:
+            o, i = v("bt%d" % t, b, 512, 4), ind(v("g%d" % t, 384 * b, 384 * b + 384), v("src16"))
+            if q == "S":
+                act(o, i, F.Copy, scale=2.0)
+            else:
+                ts(o, i, 2.0, A.mult)
+
+    def send_border(t):
         quant("b%d" % t, v("bt%d" % t), 128)
         send(T["qf%d" % (t + 1)][:, 0:128].bitcast(dt.uint8), T["qb%d" % t][:, 0:128].bitcast(dt.uint8), "rb%d" % t, v("qb%d" % t)[1])
         send(T["sf%d" % (t + 1)][:], T["sb%d" % t][:], "rb%d" % t, v("sb%d" % t)[1])
         for n in ("qf%d", "sf%d"):
             hist[n % (t + 1)] = [(0, 128, True, "R", "rb%d" % t, 2 * len(eng))]
 
-    def border_alive(t):
-        emit("V", lambda: g.vector.tensor_copy(T["alive%d" % t][:, 0:384].indirect(T.v16[:, 0:16]), T.zeros[:]),
-             v("zeros")[1] + v("v16")[1] + v("alive%d" % t)[1], v("alive%d" % t)[1])
-        scan(v("arow"), v("ones"), v("alive%d" % t), 0.0, A.mult, A.add)
-
-    def junk(n):
-        turn[0] = (turn[0] + 1) % 4
-        return v("junk", 384 * turn[0], 384 * turn[0] + n)
-
-    def border_count(t, ms, q="S"):
-        last = t == R - 1
-        thr = "thrl" if last else "thr"
-        for m in ms:
-            a = 112 - 16 * m if last else 16 * m
-            if q == "S":
-                act(junk(272), v("arow", a, a + 272), F.Sign, bias=v(thr, m, m + 1), scale=-1.0, acc=v("accb", m, m + 1))
-            else:
-                turn[1] = (turn[1] + 1) % 3
-                o = v("ltb", 272 * turn[1], 272 * turn[1] + 272)
-                ts(o, v("arow", a, a + 272), v(thr, m, m + 1), A.is_lt, 2.0, A.mult)
-                scan(v("cs", 272 * m, 272 * m + 272), v("ones", 0, 272), o, -272.0, A.mult, A.add)
-
-    def border_columns(t):
-        n, c2 = (NLAST, "c2l") if t == R - 1 else (NMID, "c2")
-        yield tt(v("sb_", n, 8), v("cs", 272 * n + 271, 2176, 272), v(c2, n, 8), A.add)
-        yield tt(v("sb_", 0, n), v("accb", 0, n), v(c2, 0, n), A.add)
-        if t == 0:
-            yield ts(v("sa_"), v("sb_"), 255.5, A.is_ge, 0.5, A.mult)
-            yield ts(v("sc_"), v("sb_"), -0.5, A.mult, 127.0, A.add)
-            yield tt(v("sa_"), v("sa_"), v("sb_"), A.mult)
-            yield tt(v("sf_"), v("sa_"), v("sc_"), A.max)
-            yield cp(v("src16"), v("sf_"))
-        else:
-            yield ts(v("src16"), v("sb_"), 0.5, A.mult)
-
-    def border_names(t):
-        yield tt(v("mn"), ind(v("trw%d" % t), v("src16")), v("diag", 0, 128), A.mult)
-        yield scan(v("mh"), v("keep", 0, 128), v("mn"), 0.0, A.mult, A.add)
-        yield cp(v("sa%d" % t), v("mh", 15, 128, 16))
-        send_names(t)
-
-    def border_list(t):
-        yield from border_columns(t)
-        yield from border_names(t)
-
-    def border_gather(t, b, q):
-        o, i = v("bt%d" % t, b, 512, 4), ind(v("g%d" % t, 384 * b, 384 * b + 384), v("src16"))
-        if q == "S":
-            act(o, i, F.Copy, scale=2.0)
-        else:
-            ts(o, i, 2.0, A.mult)
-
-    for t in range(R):
-        tr = "trw%d" % t
-        ts(v("bits", 0, 512, 4), ps(0, 128), 0.0, A.is_lt)
-        ts(v("bits", 1, 512, 4), ps(1, 128), 0.0, A.is_lt)
-        quant("bit", v("bits"), 128)
-        mm(2, 128, "n", 0, "bit")
-        mm(3, 128, "n", 128, "bit")
-        if t > 0:
-            decode_x(t, range(4))
-            border_count(t - 1, range(NMID, 8), "V")
-        else:
-            cp(v("la0"), v("nmi"))
-            names_in(0)
-            cp(v("lm"), v("im"))
-        for hf in (0, 1):
-            a, e = 128 * hf, 128 * hf + 128
-            tt(v("hm", a, e), ps(2 + hf, 128), v("diag", a, e), A.mult)
-            act(v(tr, 128 + a, 128 + e), ps(2 + hf, 128), F.Copy)
-        if t > 0:
-            border_count(t - 1, range(NEARLY, NMID))
-        scan(v("hold"), v("keep"), v("hm"), 0.0, A.mult, A.add)
-        if t == 0:
-            for b in range(4):
-                act(v("ctile", 512 * b + b, 512 * b + 512, 4), v("idn"), F.Copy)
-            ts(v("base"), v("base0"), v("kap"), A.add)
-            ts(v("k1"), v("kap"), 1.5, A.add)
-            ts(v("e1"), v("kap"), 16.0 * MS + 16.0, A.mult, 255.0 - 16.0 * MS, A.add)
-            ts(v("e3"), v("kap"), -16.0 * MS, A.mult, 255.0 + 16.0 * MS * MS, A.add)
-            ts(v("e2"), v("kap"), float(S2), A.add)
-            ts(v("sel1"), v("kap"), 0.5, A.is_ge)
-            tt(v("k2"), v("k1"), v("k1"), A.mult)
-            tt(v("pe"), v("e1"), v("e3"), A.min)
-            ts(v("sel2"), v("kap"), MS - 0.5, A.is_lt, v("sel1"), A.mult)
-            ts(v("ends"), v("k2"), 8.0, A.mult, -3.0, A.add)
-            ts(v("pr"), v("pe"), v("e2"), A.subtract, v("sel2"), A.mult)
-            fill(v("bm64"), -64.0)
-            ts(v("ends2"), v("pr"), v("e2"), A.add)
-        else:
-            copy_x(t, range(4))
-        steps = border_list(t - 1) if t > 0 else iter(())
-        for m in range(16):
-            ts(v("qq", off1(m), off1(m + 1)), v(tr, 128, 144 + 16 * m), v("hold", 16 * m + 15, 16 * m + 16), A.not_equal, 1024.0, A.mult)
-            if m >= LSTEP:
-                next(steps, None)
-        cp(v("nw16"), v("hold", 15, 256, 16))
+    def run(steps):
         for x in steps:
             pass
+
+    dma("Y", T.xin[:], T.x[:], [], v("xin")[1])
+    dma("S", T.uin[:], T.u[:], [], v("uin")[1])
+    dma("Y", T.nmi[:], T.nm[:], [], v("nmi")[1])
+    dma("S", T.hin[:], T.h[:], [], v("hin")[1])
+    dma("Y", T.qw[:, 0:512].bitcast(dt.uint8), T.wc[:, 0:2048], [], v("qw")[1])
+    dma("S", T.sw[:], T.ws[:], [], v("sw")[1])
+    dma("Y", T.vin[:], T.v[:], [], v("vin")[1])
+
+    iota(v("qi"), [[0, 1]], 0, 1, small=False)
+    iota(v("o16"), [[1, 18]])
+    fill(v("blk"), 1.0)
+    fill(v("ntile"), 0.0)
+    keep_where(v("blk"), [[-16, 8], [0, 16]], A.is_ge, 0, 1)
+    keep_where(v("blk"), [[16, 8], [0, 16]], A.is_ge, 15, -1)
+    iota(v("r16"), [[0, 8], [1, 16]])
+    iota(v("plc"), [[-64, 128]], 64 * 127)
+    emit("V", lambda: g.vector.tensor_scalar(T.qi2[:], T.qi[:], 15, None, A.bitwise_and), v("qi")[1], v("qi2")[1])
+    act(v("bits0"), v("ntile"), F.Copy)
+    act(v("bits1"), v("ntile"), F.Copy)
+    fill(v("tiny", 0, 32), 0.0)
+    cp(v("kap"), v("qi2"))
+    fill(v("tm1"), -1.0)
+    fill(v("tm2"), 1.0)
+    ts(v("pe16"), v("o16", 0, 16), v("kap"), A.is_lt, 1.0, A.add)
+    ts(v("k1"), v("kap"), 1.0, A.add)
+    scan(v("pwv"), v("pe16"), v("pe16"), 1.0, A.mult, A.max)
+    ts(v("tm1", 0, 18), v("o16"), v("k1"), A.is_equal, 2049.0, A.mult)
+    ts(v("pw"), v("kap"), 6.5, A.is_lt, v("pwv", 15, 16), A.mult)
+    ts(v("tm1", 0, 18), v("tm1", 0, 18), -1.0, A.add)
+    ts(v("ntile", 0, 512, 4), v("blk"), v("pw"), A.mult, -0.5, A.mult)
+    ts(v("tm2", 112, 128), v("o16", 0, 16), v("kap"), A.is_equal, 63.0, A.mult)
+    for m in range(8):
+        act(v("inc", off1(m), off1(m + 1)), v("tm1", 0, 129 - 16 * m), F.Copy)
+    quant("n", v("ntile"), 128)
+    ts(v("tm2", 112, 128), v("tm2", 112, 128), 1.0, A.add)
+    fill(v("ctile"), 1.0)
+    ts(v("sta"), v("r16"), v("k1"), A.is_equal, O1, A.mult)
+    ts(v("st1"), v("r16"), v("kap"), A.is_equal, 1024.0, A.mult)
+    keep_where(v("ctile"), [[1, 516]], A.is_equal, -3, -4)
+    iota(v("row", 128, 288, 144), [[0, 2]], -1)
+    iota(v("iota"), [[64, 256]])
+    iota(v("vh", 128, 384), [[0, 256]])
+    iota(v("nms"), [[1, 128]])
+    quant("u", v("uin"), 128)
+    tt(v("st1"), v("st1"), v("sta"), A.add)
+    ts(v("n1"), v("kap"), 14.5, A.is_lt, -O1, A.mult)
+    ts(v("k8"), v("kap"), 7.0, A.min)
+    ts(v("nb"), v("n1"), -1024.0, A.mult)
+    ts(v("a1"), v("k8"), -8.0, A.mult, 121.0, A.add)
+    ts(v("a2"), v("k8"), 8.0, A.mult, 24.0, A.add)
+    for h in (0, 1):
+        quant("x0", v("xin", 512 * h, 512 * h + 512), 128, 128 * h)
+        scores(0, h)
+    signs(0)
+    cp(v("la0"), v("nmi"))
+    ts(v("ends1"), v("a1"), v("k8"), A.mult, 128.0, A.add)
+    names(0)
+    signs(1)
+    ts(v("ends2"), v("a2"), v("k8"), A.mult, 15.0, A.add)
+    names(1)
+    name_row(0)
+    scatter(v("w0", 128, 256), v("la0"), v("plc"))
+    name_row(1)
+    wrap(0)
+    wrap(1)
+    wrapped(0)
+    compare(0, "S")
+    compare(0, "V")
+    look_up(0)
+    wrapped(1)
+    for n, c in (("2", 128.0), ("3", 256.0)):
+        act(v("st" + n), v("st1"), F.Copy, scale=c)
+        act(v("n" + n), v("n1"), F.Copy, scale=c)
+    act(v("n2b"), v("n1"), F.Copy, scale=128.0)
+    for m in range(8):
+        act(v("keep", off2(m), off2(m + 1)), v("tm2", 112 - 16 * m, 128), F.Copy)
+    next_use(0)
+    quant("e", v("ctile", 3, 515), 128, 0)
+    steps = places(0)
+    for b in range(1, 4):
+        next(steps, None)
+        quant("e", v("ctile", 3 - b, 515 - b), 128, 128 * b)
+    for m in range(8):
+        act(v("keep", off2(m), off2(m) + 1), v("o16", 0, 1), F.Copy)
+    act(v("cs"), v("n1"), F.Identity, scale=256.0, bias=8192.0)
+
+    for t in range(R):
+        if t > 0:
+            new_x(t, 0)
+            scores(t, 0)
+            copy_y(1, (0, 1))
+            signs(0)
+            copy_y(1, (2, 3))
+            decode_x(t, 0, (0, 1, 2))
+            src = sources(t - 1)
+            next(src)
+            names(0)
+            next(src)
+            new_x(t, 1)
+            next(src)
+            scores(t, 1)
+            name_row(0)
+            copy_x(t, 0, (0, 1))
+            decode_x(t, 1, (0, 1))
+            decode_x(t, 0, (3,))
+            signs(1)
+            wrap(0)
+            table(t, 0)
+            decode_x(t, 1, (2, 3))
+            wrapped(0)
+            compare(0, "S")
+            compare(0, "V")
+            names(1)
+            look_up(0)
+            copy_x(t, 0, (2, 3))
+            name_row(1)
+            copy_x(t, 1, range(4))
+            next_use(0)
+            pl = places(0)
+            next(pl)
+            wrap(1)
+            next(pl)
+            wrapped(1)
+            border(t - 1, range(4))
+        else:
+            compare(1, "S")
+        latest(0)
         if t == 0:
             quant("f0", v("hin"), 128)
-        else:
-            for b in range(4):
-                border_gather(t - 1, b, "S")
-        scan(v("sc"), v("inc"), v("qq"), 0.0, A.add, A.min)
+        compare(1, "V")
+        last_uses(0)
+        wrap_latest(0)
         if t > 0:
-            border_send(t - 1)
-        else:
-            quant("e", v("ctile"), 512)
-            decode_x(0, range(4))
-            copy_x(0, range(4))
-        ts(v("nh"), ind(v("sc"), v("ends")), -0.5, A.is_ge, 1024.0, A.mult)
-        tt(v("x1"), ind(v("sc"), v("ends")), v("base"), A.subtract)
-        if t > 0:
-            names_in(t)
-        names_row(t)
-        tt(v("pl"), ind(v("pt%d" % t), v("nw16")), v("diag"), A.mult)
-        tt(v("w1"), v("x1"), v("nh"), A.add)
-        scan(v("plh"), v("keep"), v("pl"), 0.0, A.mult, A.add)
-        tt(v("w"), v("w1"), v("plh", 15, 256, 16), A.min)
-        ts(v("v16"), v("w"), -1.0, A.mult, 128.0, A.add)
-        act(v("vw"), v("w"), F.Copy, scale=-1.0)
-        act(v("e32", 0, 16), v("w"), F.Identity, bias=v("bm64"), scale=64.0)
-        cp(v("vr"), ind(v("iota"), v("v16")))
+            send_border(t - 1)
+            compare(1, "S")
+        ranks(0)
         if t == 0:
-            ts(v("keep2", 0, 256), v("diag"), 63.0, A.mult, 1.0, A.add)
-            fill(v("keep2", 0, 256, 16), 0.0)
-            fill(v("keep2", 256, S2, 16 * MS), 0.0)
-            fill(v("keep2", 272, S2, 16 * MS + 16), 0.0)
-        for m in range(MS, 16):
-            act(junk(16 * m), v("vr", 0, 16 * m), F.Sign, bias=v("vw", m, m + 1), scale=-1.0, acc=v("acc", m, m + 1))
-        act(v("e32", 16 + MS, 32), v("acc", MS, 16), F.Copy, scale=32.0)
-
-        def shorter(a, b):
-            for m in range(a, b):
-                ts(v("lt", off2(m), off2(m) + 16 * m), v("vr", 0, 16 * m), v("vw", m, m + 1), A.is_lt, 64.0, A.mult)
-
-        tt(v("lt", 0, 256), ind(v("vw"), v("lm")), v("vr"), A.is_gt)
-        shorter(1, 4)
-        scan(v("sc2", 0, 256), v("keep2", 0, 256), v("lt", 0, 256), 0.0, A.mult, A.add)
-        shorter(4, MS)
-        tt(v("dd"), v("sc2", 15, 256, 16), v("e32", 0, 16), A.add)
-        scan(v("sc2", 256, S2), v("keep2", 256, S2), v("lt", 256, S2), 0.0, A.mult, A.add)
-        tt(v("dd", MS, 16), v("dd", MS, 16), v("e32", 16 + MS, 32), A.add)
-        tt(v("d"), ind(v("sc2"), v("ends2")), v("dd"), A.add)
-        if t == 0:
-            ts(v("d16"), v("d"), 1.0 / 64, A.mult)
-        else:
-            ts(v("d16"), v("d"), -1.0 / 64, A.mult, 127.0, A.add)
+            for h in (0, 1):
+                decode_x(0, h, range(4))
+                copy_x(0, h, range(4))
+        counts(0)
+        next_use(1)
+        count_sums(0)
+        for x in zip(places(1), distance(0)):
+            pass
+        rank_list(t, 0)
+        table(t, 1)
+        look_up(1)
+        hand_on()
+        latest(1)
+        last_uses(1)
+        wrap_latest(1)
         decode_f(t)
-        for hf in (0, 1):
-            a, e = 128 * hf, 128 * hf + 128
-            for b in range(4):
-                tt(v("zt", 4 * a + b, 4 * e, 4), ind(front_of(t, b), v("d16", 8 * hf, 8 * hf + 8)), x_of(t, b, a, e), A.add)
-            quant("z", v("zt", 4 * a, 4 * e), 128, a)
-            for b in range(4):
-                mm(4 * hf + b, 128, "w", 128 * b, "z", a)
-        if t == 0:
-            ts(v("thr"), v("thr0"), v("kap"), A.add, 0.5, A.add)
-        border_alive(t)
-        if t == 0:
-            ts(v("thrl"), v("thr"), -1.0, A.mult, 128.0, A.add)
-            fill(v("b127"), 127.0)
-        for hf in (0, 1):
-            a, e = 128 * hf, 128 * hf + 128
-            for b in range(4):
-                if hf == 1 and b >= YV:
-                    ts(v("yt", 4 * a + b, 4 * e, 4), ps(4 * hf + b, 128), 0.03125, A.mult)
-                else:
-                    act(v("yt", 4 * a + b, 4 * e, 4), ps(4 * hf + b, 128), F.Copy, scale=0.03125)
-            quant("x%d" % (t + 1), v("yt", 4 * a, 4 * e), 128, a)
-            if t < R - 1:
-                mm(hf, 128, "u", 0, "x%d" % (t + 1), a)
+        copy_f(t)
+        ranks(1)
+        counts(1)
+        count_sums(1)
+        mix(t, 0)
+        run(distance(1))
+        layer(0)
+        rank_list(t, 1)
         if t < R - 1:
-            border_count(t, range(NEARLY))
+            send_ranks(t)
+        copy_y(0)
+        mix(t, 1)
+        layer(1)
 
-    decode_x(R, range(4))
-    border_count(R - 1, range(NLAST))
-    border_count(R - 1, range(NLAST, 7), "V")
-    copy_x(R, (0, 1, 3))
-    copy_x(R, (2,), "V")
-    border_count(R - 1, (7,), "V")
-    for x in border_columns(R - 1):
-        pass
-    for b in (0, 1):
-        border_gather(R - 1, b, "S")
-    for b in (2, 3):
-        border_gather(R - 1, b, "V")
-    border_send(R - 1)
-    for x in border_names(R - 1):
-        pass
+    new_x(R, 0)
+    decode_x(R, 0, range(4))
+    copy_y(1, (0, 1))
+    run(sources(R - 1))
+    copy_y(1, (2, 3), "V")
+    copy_x(R, 0, range(4))
+    new_x(R, 1)
+    decode_x(R, 1, range(4))
+    copy_x(R, 1, (0, 1))
+    copy_x(R, 1, (2, 3), "V")
+    border(R - 1, (0, 1))
+    border(R - 1, (2, 3), "V")
+    send_border(R - 1)
+    send_ranks(R - 1)
     quant("v", v("vin"), 128)
     mm(1, 256, "v", 0, "x3")
     act(v("ysb", 0, 256), ps(1, 256), F.Copy)
-    act(v("olb", 0, 256), ind(v("iotap"), v("d16")), F.Identity, bias=v("b127"), scale=-1.0)
+    act(v("olb", 0, 256), ind(v("iota", 0, 128), v("d16")), F.Identity, bias=127.0, scale=-1.0 / 64)
 
     def stores(a, n, q, s):
         dma("Y", T.oc[:, 4 * a:4 * (a + n)], T[q][:, 0:n].bitcast(dt.uint8), v(q)[1], [])
@@ -496,7 +539,7 @@ def rank_program(g, core, T, topo):
     cp(v("ysb", 256, 384), ps(2, 128))
     stores(256, 128, "qf3", "sf3")
     dma("Y", T.y[:, 256:384], T.ysb[:, 256:384], v("ysb", 256, 384)[1], [])
-    act(v("olb", 256, 384), ind(v("iotap"), v("la3")), F.Copy)
+    scatter(v("olb", 256, 384), v("la3"), v("nms"))
     dma("S", T.ol[:, :], T.olb[0:128:16, :], v("olb")[1], [])
 
     for s in ("cv", "cs", "cp", "cg"):

@@ -1,19 +1,43 @@
 from concourse.mybir import dt, AluOpType as A, ActivationFunctionType as F
 
 C, K, R = 256, 128, 3
-NS = 0
-O1 = -128.0
+EPS = 1.0 / 1024
+O1 = -128.0 * EPS
+
+FIRST = """load_x 0, load_u, load_x 1, load_nm, load_h, load_w, load_ws, load_v, lane, o16, blk, ntile0, tm1, lane_low, tm2, bits0 0, kap, bits0 1,
+ones, diagonal, k1, tm1a, tm1b, sta, stb, pe16, lane_high, st1, pwv, grp, dummy, plc, hold0, iota, vh0, nms, n1, pw, ntile, tm2a, a2, a3,
+st1a, a4, m1, st1b, inc, a1, c1, la0, ends2, quant_u, new_x 0, quant_n, st1c, inc_a, scores 0, new_x 1, scores 1, n2b, signs 0, n1b, st2, st3,
+quant_e 0, quant_e 1, quant_e 2, names 0, signs 1, first_table, names 1, cs, name_row 0, inc_b, wrap 0, keep, name_row 1, quant_e 3,
+compare 0 0, compare 0 1, ends1, wrapped 0, look_up 0, n2, next_use 0, wrap 1, place 0, wrapped 1, place_list 0, decode_x 0 0 1 2 3,
+copy_x 0 0, copy_x 0 1, copy_x 0 2, copy_x 0 3, decode_x 1 0 1 2 3, latest 0, last_uses 0, quant_h, copy_x 1 0, copy_x 1 1, compare 1 0,
+compare 1 1, wrap_latest 0, rank_start 0, keep_a, ranks 0 0, ranks 0 1, keep_b, next_use 1, counts 0 1, counts 0 0, place 1, rank_list 0,
+quant_v, count_sums 0, distance 0, place_list 1, hand_on, table 1, look_up 1, copy_x 1 2, copy_x 1 3, n3, distance_list 0, latest 1,
+wrap_latest 1, last_uses 1, decode_f, copy_f 0, copy_f 1, copy_f 2, rank_start 1, copy_f 3, ranks 1 0, ranks 1 1, counts 1 1, counts 1 0,
+mix 0 0, count_sums 1, mix 0 1, mix 0 2, mix 0 3, distance 1, layer 0, distance_list 1, rank_list 1, send_ranks, copy_y 0 0, copy_y 0 1,
+copy_y 0 2, copy_y 0 3, mix 1 0, mix 1 1, mix 1 2, mix 1 3, layer 1"""
+ROUND = """new_x 0, scores 0, copy_y 1 0, copy_y 1 1, copy_y 1 2, signs 0, decode_x 0 0 1, decode_x 0 2, sources, copy_y_v 1 3, wrap_sources,
+names 0, new_x 1, source_list, scores 1, copy_x 0 0, copy_x 0 1, decode_x 1 0 1, copy_x 0 2, name_row 0, decode_x 0 3, signs 1, wrap 0,
+decode_x 1 2, compare 0 1, names 1, decode_x 1 3, copy_x 1 0, copy_x 1 1, border 0, border 1, table 0, compare 0 0, wrapped 0, name_row 1,
+look_up 0, copy_x 0 3, copy_x 1 3, copy_x 1 2, next_use 0, place 0, place_list 0, wrap 1, border 3, border 2, latest 0, last_uses 0,
+compare 1 1, send_border, wrapped 1, compare 1 0, wrap_latest 0, rank_start 0, ranks 0 0, ranks 0 1, counts 0 1, counts 0 0, next_use 1,
+rank_list 0, count_sums 0, place 1, distance 0, place_list 1, distance_list 0, hand_on, table 1, look_up 1, latest 1, wrap_latest 1,
+last_uses 1, decode_f, rank_start 1, copy_f 0, copy_f 1, copy_f 2, copy_f 3, ranks 1 0, ranks 1 1, counts 1 1, counts 1 0, count_sums 1,
+mix 0 0, mix 0 1, mix 0 2, distance 1, mix 0 3, distance_list 1, layer 0, copy_y 0 1, copy_y 0 2, mix 1 0, mix 1 1, mix 1 2, mix 1 3,
+rank_list 1, send_ranks, copy_y 0 0, copy_y 0 3, layer 1"""
+LAST = """sources, new_x 0, decode_x 0 0 1 2 3, copy_y 1 0, copy_y 1 1, copy_y_v 1 2, copy_y_v 1 3, copy_x 0 0, copy_x 0 1, copy_x 0 2, copy_x 0 3,
+new_x 1, wrap_sources, source_list, decode_x 1 0 1 2 3, copy_x 1 0, copy_x 1 1, copy_x_v 1 2, copy_x_v 1 3, border 0, border 1, border_v 2,
+border_v 3, send_border, y_x, ol_d, store_y 0, stores 0, ol_a, store_ol, y_f, stores 1, store_y 1"""
 
 
 def off1(m):
-    return 129 * m - 8 * m * (m - 1)
+    return 146 * m if m < 4 else 146 * (7 - m) + 17 + 16 * m
 
 
 def off2(m):
-    return 8 * m * (m + 1)
+    return 144 * m if m < 4 else 144 * (7 - m) + 128 - 16 * m
 
 
-S1, S2 = off1(8), off2(8)
+S1, S2 = 4 * 146, 4 * 144
 BF, F32, I32, U16, U8, Q8 = "bfloat16", "float32", "int32", "uint16", "uint8", "float8_e4m3fn_x4"
 SCRATCH, TINY = {}, {}
 
@@ -23,19 +47,19 @@ def buf(name, n, d=BF, where="sbuf"):
 
 
 for _n, _w in (("xin", 1024), ("hin", 512), ("uin", 512), ("vin", 512), ("bits0", 512), ("bits1", 512), ("ctile", 516), ("ntile", 512),
-               ("zt", 1024), ("yt", 1024), ("blk", 128), ("o16", 18), ("pe16", 16), ("r16", 128), ("st1", 128), ("st2", 128), ("st3", 128),
-               ("sta", 128), ("tm1", 130), ("tm2", 128), ("inc", S1), ("keep", S2), ("iota", 256), ("plc", 128), ("nms", 128), ("row", 288),
-               ("hold", 256), ("qq0", S1), ("qq1", S1), ("sc0", S1), ("sc1", S1), ("w0", 256), ("w1", 256), ("r1", 128), ("vh", 384),
-               ("lh0", 128), ("lt0", S2), ("lt1", S2), ("cs0", S2), ("cs1", S2), ("junk", 512), ("srow", 128), ("gx", 1536), ("n2b", 1)):
+               ("zt", 1024), ("yt", 1024), ("blk", 128), ("o16", 18), ("pe16", 16), ("st1", 128), ("st2", 128), ("st3", 128),
+               ("sta", 16), ("stb", 16), ("tm1", 130), ("tm2", 128), ("inc", S1), ("keep", S2), ("iota", 256), ("plc", 128), ("nms", 128),
+               ("row", 288), ("hold", 384), ("qq0", S1), ("qq1", S1), ("sc0", S1), ("sc1", S1), ("w0", 256), ("w1", 256), ("r1", 128),
+               ("vh", 384), ("lh0", 128), ("lt0", S2), ("lt1", S2), ("cs0", S2), ("cs1", S2), ("junk", 512), ("srow", 128), ("gx", 1536),
+               ("n1b", 1), ("n2b", 1)):
     buf(_n, _w)
-for _n, _w in (("nw0", 16), ("nw1", 16), ("kap", 1), ("pw", 1), ("k1", 1), ("k8", 1), ("a1", 1), ("a2", 1), ("n1", 1), ("n2", 1), ("n3", 1), ("nb", 1),
-               ("cs", 1), ("pwv", 16), ("nb0", 8), ("nb1", 8), ("x0", 16), ("x1", 16), ("y0", 16), ("y1", 16), ("lw0", 8), ("lw1", 8),
-               ("acc0", 8), ("acc1", 8)):
+for _n, _w in (("kap", 1), ("grp", 1), ("pw", 1), ("k1", 1), ("a1", 1), ("a2", 1), ("a3", 1), ("a4", 1), ("n1", 1), ("n2", 1), ("n3", 1), ("m1", 1),
+               ("c1", 1), ("cs", 1), ("pwv", 16), ("x0", 16), ("x1", 16), ("y0", 16), ("y1", 16), ("lw0", 8), ("lw1", 8), ("acc0", 8), ("acc1", 8)):
     TINY[_n] = (sum(w for o, w in TINY.values()), _w)
 buf("tiny", sum(w for o, w in TINY.values()), F32)
 for _n, _w in (("ysb", 384), ("olb", 384), ("lh1", 128), ("sh", 128)):
     buf(_n, _w, F32)
-for _n, _w in (("qi", 1), ("qi2", 1), ("nmi", 8)):
+for _n, _w in (("qi", 1), ("qi2", 1), ("qi3", 1), ("nmi", 8)):
     buf(_n, _w, I32)
 for _n, _w in (("ends1", 1), ("ends2", 1), ("nw16", 16), ("off16", 16), ("d16", 16), ("src16", 8), ("la0", 8), ("lm", 8)):
     buf(_n, _w, U16)
@@ -53,7 +77,7 @@ for _n, _w in (("u", 128), ("v", 128), ("w", 512), ("e", 512), ("n", 128), ("bit
 for _n in range(8):
     buf("p%d" % _n, 512, F32, "psum")
 
-NDMA = 22
+NDMA = 21
 SEMAPHORES = ["cv", "cs", "cp", "cg", "left"] + ["ra%d" % t for t in range(R)] + ["rb%d" % t for t in range(R)] + ["d%d" % i for i in range(NDMA)]
 
 
@@ -155,7 +179,7 @@ def rank_program(g, core, T, topo):
             w += acc[1]
         emit("S", lambda: g.scalar.activation(o[0], a[0], func, **kw), r, w)
 
-    def quant(name, src, n, a=0):
+    def quant(name, src, n=128, a=0):
         q, s = v("q" + name, a, a + n), v("s" + name, a, a + n)
         emit("V", lambda: g.vector.quantize_mx(q[0], s[0], src[0]), src[1], q[1] + s[1])
 
@@ -194,121 +218,118 @@ def rank_program(g, core, T, topo):
     def front_of(t, b):
         return v("g%d" % t, 384 * b, 384 * b + 128)
 
+    def held(name, h, n=8):
+        return v(name, 128 * h + 15, 128 * h + 16 * n, 16)
+
+    def new_x(t, h):
+        quant("x%d" % t, v("yt" if t else "xin", 512 * h, 512 * h + 512), 128, 128 * h)
+
     def scores(t, h):
         mm(4 * h, 128, "u", 0, "x%d" % t, 128 * h)
 
-    def signs(h):
+    def signs(t, h):
         act(v("bits%d" % h, 0, 512, 4), ps(4 * h, 128), F.Sign, bias=2.0 ** -100)
 
-    def names(h):
-        quant("bit%d" % h, v("bits%d" % h), 128)
+    def names(t, h):
+        quant("bit%d" % h, v("bits%d" % h))
         mm(4 * h + 1, 128, "n", 0, "bit%d" % h)
 
-    def name_row(h):
-        act(v("row", 144 * h, 144 * h + 128), ps(4 * h + 1, 128), F.Identity, bias=63.5)
+    def name_row(t, h):
+        act(v("row", 144 * h, 144 * h + 128), ps(4 * h + 1, 128), F.Identity, bias=63.5 * EPS, scale=EPS)
 
-    def wrap(h):
+    def wrap(t, h):
         scan(v("hold", 128 * h, 128 * h + 128), v("st1"), v("row", 144 * h, 144 * h + 128), 0.0, A.add, A.min)
 
-    def wrapped(h):
-        held = v("hold", 128 * h + 15, 128 * h + 128, 16)
-        ts(v("nw%d" % h, 0, 8), held, v("n1"), A.add)
-        ts(v("nw16", 8 * h, 8 * h + 8), held, v("n1"), A.add)
-        if NS:
-            act(v("nb%d" % h), held, F.Identity, bias=v("nb"), scale=-1024.0)
+    def wrapped(t, h):
+        ts(v("nw16", 8 * h, 8 * h + 8), held("hold", h), v("n1"), A.add, 1 / EPS, A.mult)
 
-    def compare(h, q):
-        for m in (range(8 - NS) if q == "V" else range(8 - NS, 8)):
-            o, i = v("qq%d" % h, off1(m), off1(m + 1)), v("row", 144 * h + 16 * m, 144 * h + 129)
-            if q == "V":
-                ts(o, i, v("nw%d" % h, m, m + 1), A.not_equal, 1024.0, A.mult)
-            else:
-                act(o, i, F.Abs, bias=v("nb%d" % h, m, m + 1), scale=1024.0)
+    def compare(t, h, k):
+        for m in range(4 * k, 4 * k + 4):
+            c = 128 * h + 16 * m + 15
+            ts(v("qq%d" % h, off1(m), off1(m) + 129 - 16 * m), v("row", 144 * h + 16 * m, 144 * h + 129), v("n1b"), A.subtract,
+               v("hold", c, c + 1), A.not_equal)
 
-    def next_use(h):
+    def next_use(t, h):
         scan(v("sc%d" % h), v("inc"), v("qq%d" % h), 0.0, A.add, A.min)
 
-    def places(h):
-        yield tt(v("x%d" % h), ind(v("sc%d" % h), v("ends1")), v("nw%d" % h), A.min)
-        yield ts(v("off16", 8 * h, 8 * h + 8), v("x%d" % h, 0, 8), 128.0, A.add)
+    def place(t, h):
+        tt(v("x%d" % h), ind(v("sc%d" % h), v("ends1")), held("hold", h, 16), A.min)
+
+    def place_list(t, h):
+        ts(v("off16", 8 * h, 8 * h + 8), v("x%d" % h, 0, 8), v("c1"), A.add, 1 / EPS, A.mult)
 
     def table(t, h):
         act(v("r1") if h else v("w0", 128, 256), ind(v("iota", 0, 128), v("lm" if h else "la%d" % t)), F.Copy)
 
-    def look_up(h):
+    def look_up(t, h):
         act(v("w%d" % h, 0, 128), ind(v("r1") if h else v("w0", 128, 256), v("nw16", 8 * h, 8 * h + 8)), F.Copy)
 
-    def hand_on():
+    def hand_on(t):
         act(v("w1", 128, 256), v("w0", 128, 256), F.Identity, bias=-8192.0)
 
-    def latest(h):
+    def latest(t, h):
         scatter(v("w%d" % h), v("off16", 8 * h, 8 * h + 8), v("iota", 128, 256))
 
-    def wrap_latest(h):
+    def wrap_latest(t, h):
         scan(v("vh", 128 * h, 128 * h + 128), v("st2"), v("w%d" % h, 0, 128), 0.0, A.add, A.min)
 
-    def counts(h):
-        for m in range(7, -1, -1):
+    def counts(t, h, k):
+        for m in range(4 * k, 4 * k + 4):
             c = 128 * h + 16 * m + 15
-            ts(v("lt%d" % h, off2(m), off2(m + 1)), v("w%d" % h, 0, 16 * m + 16), v("n2b"), A.subtract, v("vh", c, c + 1), A.is_lt)
+            ts(v("lt%d" % h, off2(m), off2(m) + 16 * m + 16), v("w%d" % h, 0, 16 * m + 16), v("n2b"), A.subtract, v("vh", c, c + 1), A.is_lt)
 
-    def count_sums(h):
+    def count_sums(t, h):
         scan(v("cs%d" % h), v("keep"), v("lt%d" % h), 0.0, A.mult, A.add)
 
-    def distance(h):
-        yield tt(v("y%d" % h), ind(v("cs%d" % h), v("ends2")), v("vh", 128 * h + 15, 128 * h + 256, 16), A.subtract)
-        yield ts(v("d16", 8 * h, 8 * h + 8), v("y%d" % h, 0, 8), v("n2"), A.subtract, -1.0 / 64, A.mult)
+    def distance(t, h):
+        tt(v("y%d" % h), ind(v("cs%d" % h), v("ends2")), held("vh", h, 16), A.subtract)
+
+    def distance_list(t, h):
+        ts(v("d16", 8 * h, 8 * h + 8), v("y%d" % h, 0, 8), v("n2"), A.subtract, -1.0 / 64, A.mult)
 
     def decode_f(t):
         for b in range(4):
             mm(b, 128, "e", 128 * b, "f%d" % t)
 
-    def copy_f(t):
-        for b in range(4):
-            i = ps(b, 128) if t else (T["p%d" % b][:, 127::-1], ps(b, 128)[1])
-            act(front_of(t, b), i, F.Copy, scale=0.5)
+    def copy_f(t, b):
+        i = ps(b, 128) if t else (T["p%d" % b][:, 127::-1], ps(b, 128)[1])
+        act(front_of(t, b), i, F.Copy, scale=0.5)
 
-    def mix(t, h):
-        a, e = 128 * h, 128 * h + 128
-        for b in range(4):
-            tt(v("zt", 4 * a + b, 4 * e, 4), ind(front_of(t, b), v("d16", 8 * h, 8 * h + 8)), x_of(t, b, h), A.add)
+    def mix(t, h, b):
+        tt(v("zt", 512 * h + b, 512 * h + 512, 4), ind(front_of(t, b), v("d16", 8 * h, 8 * h + 8)), x_of(t, b, h), A.add)
 
-    def layer(h):
+    def layer(t, h):
         quant("z", v("zt", 512 * h, 512 * h + 512), 128, 128 * h)
         for b in range(4):
             mm(4 * h + b, 128, "w", 128 * b, "z", 128 * h)
 
-    def copy_y(h, planes=range(4), q="S"):
-        for b in planes:
-            o = v("yt", 512 * h + b, 512 * h + 512, 4)
-            if q == "S":
-                act(o, ps(4 * h + b, 128), F.Copy, scale=0.03125)
-            else:
-                ts(o, ps(4 * h + b, 128), 0.03125, A.mult)
+    def copy_y(t, h, b):
+        act(v("yt", 512 * h + b, 512 * h + 512, 4), ps(4 * h + b, 128), F.Copy, scale=0.03125)
 
-    def new_x(t, h):
-        quant("x%d" % t, v("yt", 512 * h, 512 * h + 512), 128, 128 * h)
+    def copy_y_v(t, h, b):
+        ts(v("yt", 512 * h + b, 512 * h + 512, 4), ps(4 * h + b, 128), 0.03125, A.mult)
 
     def xbank(h, b):
         return ((2, 3, 0, 1), (6, 7, 4, 2))[h][b]
 
-    def decode_x(t, h, planes):
+    def decode_x(t, h, *planes):
         for b in planes:
             mm(xbank(h, b), 128, "e", 128 * b, "x%d" % t, 128 * h)
 
-    def copy_x(t, h, planes, q="S"):
-        for b in planes:
-            if q == "S":
-                act(x_of(t, b, h), ps(xbank(h, b), 128), F.Copy, scale=0.5)
-            else:
-                ts(x_of(t, b, h), ps(xbank(h, b), 128), 0.5, A.mult)
+    def copy_x(t, h, b):
+        act(x_of(t, b, h), ps(xbank(h, b), 128), F.Copy, scale=0.5)
 
-    def last_uses(h):
+    def copy_x_v(t, h, b):
+        ts(x_of(t, b, h), ps(xbank(h, b), 128), 0.5, A.mult)
+
+    def last_uses(t, h):
         scan(v("lh%d" % h), v("st3" if h else "st2"), v("w%d" % h, 128, 256), 0.0, A.add, A.min)
 
-    def ranks(h):
-        act(v("lw%d" % h), v("lh%d" % h, 15, 128, 16), F.Identity, bias=v("n3" if h else "n2"))
-        for m in range(8):
+    def rank_start(t, h):
+        act(v("lw%d" % h), held("lh%d" % h, 0), F.Identity, bias=v("n3" if h else "n2"))
+
+    def ranks(t, h, k):
+        for m in range(4 * k, 4 * k + 4):
             act(junk(), v("w%d" % h, 128, 256), F.Sign, bias=v("lw%d" % h, m, m + 1), scale=-1.0, acc=v("acc%d" % h, m, m + 1))
 
     def rank_list(t, h):
@@ -319,228 +340,146 @@ def rank_program(g, core, T, topo):
         hist["la%d" % (t + 1)] = [(0, 8, True, "R", "ra%d" % t, len(eng))]
 
     def sources(t):
-        yield scatter(v("srow"), v("sa%d" % t), v("w1", 128, 256))
-        yield scan(v("sh"), v("st3"), v("srow"), 0.0, A.add, A.min)
-        yield ts(v("src16"), v("sh", 15, 128, 16), v("cs"), A.add, 1.0 / 64, A.mult)
+        scatter(v("srow"), v("sa%d" % (t - 1)), v("w1", 128, 256))
 
-    def border(t, planes, q="S"):
-        for b in planes:
-            o, i = v("bt%d" % t, b, 512, 4), ind(v("g%d" % t, 384 * b, 384 * b + 384), v("src16"))
-            if q == "S":
-                act(o, i, F.Copy, scale=2.0)
-            else:
-                ts(o, i, 2.0, A.mult)
+    def wrap_sources(t):
+        scan(v("sh"), v("st3"), v("srow"), 0.0, A.add, A.min)
+
+    def source_list(t):
+        ts(v("src16"), held("sh", 0), v("cs"), A.add, 1.0 / 64, A.mult)
+
+    def border(t, b):
+        act(v("bt%d" % (t - 1), b, 512, 4), ind(v("g%d" % (t - 1), 384 * b, 384 * b + 384), v("src16")), F.Copy, scale=2.0)
+
+    def border_v(t, b):
+        ts(v("bt%d" % (t - 1), b, 512, 4), ind(v("g%d" % (t - 1), 384 * b, 384 * b + 384), v("src16")), 2.0, A.mult)
 
     def send_border(t):
-        quant("b%d" % t, v("bt%d" % t), 128)
-        send(T["qf%d" % (t + 1)][:, 0:128].bitcast(dt.uint8), T["qb%d" % t][:, 0:128].bitcast(dt.uint8), "rb%d" % t, v("qb%d" % t)[1])
-        send(T["sf%d" % (t + 1)][:], T["sb%d" % t][:], "rb%d" % t, v("sb%d" % t)[1])
-        for n in ("qf%d", "sf%d"):
-            hist[n % (t + 1)] = [(0, 128, True, "R", "rb%d" % t, 2 * len(eng))]
+        b, f = "b%d" % (t - 1), "f%d" % t
+        quant(b, v("bt%d" % (t - 1)))
+        send(T["q" + f][:, 0:128].bitcast(dt.uint8), T["q" + b][:, 0:128].bitcast(dt.uint8), "r" + b, v("q" + b)[1])
+        send(T["s" + f][:], T["s" + b][:], "r" + b, v("s" + b)[1])
+        for n in ("q" + f, "s" + f):
+            hist[n] = [(0, 128, True, "R", "r" + b, 2 * len(eng))]
 
-    def run(steps):
-        for x in steps:
-            pass
+    def y_x(t):
+        mm(1, 256, "v", 0, "x%d" % R)
+        act(v("ysb", 0, 256), ps(1, 256), F.Copy)
 
-    dma("Y", T.xin[:], T.x[:], [], v("xin")[1])
-    dma("S", T.uin[:], T.u[:], [], v("uin")[1])
-    dma("Y", T.nmi[:], T.nm[:], [], v("nmi")[1])
-    dma("S", T.hin[:], T.h[:], [], v("hin")[1])
-    dma("Y", T.qw[:, 0:512].bitcast(dt.uint8), T.wc[:, 0:2048], [], v("qw")[1])
-    dma("S", T.sw[:], T.ws[:], [], v("sw")[1])
-    dma("Y", T.vin[:], T.v[:], [], v("vin")[1])
+    def y_f(t):
+        mm(2, 128, "v", 0, "f%d" % R)
+        cp(v("ysb", 256, 384), ps(2, 128))
 
-    iota(v("qi"), [[0, 1]], 0, 1, small=False)
-    iota(v("o16"), [[1, 18]])
-    fill(v("blk"), 1.0)
-    fill(v("ntile"), 0.0)
-    keep_where(v("blk"), [[-16, 8], [0, 16]], A.is_ge, 0, 1)
-    keep_where(v("blk"), [[16, 8], [0, 16]], A.is_ge, 15, -1)
-    iota(v("r16"), [[0, 8], [1, 16]])
-    iota(v("plc"), [[-64, 128]], 64 * 127)
-    emit("V", lambda: g.vector.tensor_scalar(T.qi2[:], T.qi[:], 15, None, A.bitwise_and), v("qi")[1], v("qi2")[1])
-    act(v("bits0"), v("ntile"), F.Copy)
-    act(v("bits1"), v("ntile"), F.Copy)
-    fill(v("tiny", 0, 32), 0.0)
-    cp(v("kap"), v("qi2"))
-    fill(v("tm1"), -1.0)
-    fill(v("tm2"), 1.0)
-    ts(v("pe16"), v("o16", 0, 16), v("kap"), A.is_lt, 1.0, A.add)
-    ts(v("k1"), v("kap"), 1.0, A.add)
-    scan(v("pwv"), v("pe16"), v("pe16"), 1.0, A.mult, A.max)
-    ts(v("tm1", 0, 18), v("o16"), v("k1"), A.is_equal, 2049.0, A.mult)
-    ts(v("pw"), v("kap"), 6.5, A.is_lt, v("pwv", 15, 16), A.mult)
-    ts(v("tm1", 0, 18), v("tm1", 0, 18), -1.0, A.add)
-    ts(v("ntile", 0, 512, 4), v("blk"), v("pw"), A.mult, -0.5, A.mult)
-    ts(v("tm2", 112, 128), v("o16", 0, 16), v("kap"), A.is_equal, 63.0, A.mult)
-    for m in range(8):
-        act(v("inc", off1(m), off1(m + 1)), v("tm1", 0, 129 - 16 * m), F.Copy)
-    quant("n", v("ntile"), 128)
-    ts(v("tm2", 112, 128), v("tm2", 112, 128), 1.0, A.add)
-    fill(v("ctile"), 1.0)
-    ts(v("sta"), v("r16"), v("k1"), A.is_equal, O1, A.mult)
-    ts(v("st1"), v("r16"), v("kap"), A.is_equal, 1024.0, A.mult)
-    keep_where(v("ctile"), [[1, 516]], A.is_equal, -3, -4)
-    iota(v("row", 128, 288, 144), [[0, 2]], -1)
-    iota(v("iota"), [[64, 256]])
-    iota(v("vh", 128, 384), [[0, 256]])
-    iota(v("nms"), [[1, 128]])
-    quant("u", v("uin"), 128)
-    tt(v("st1"), v("st1"), v("sta"), A.add)
-    ts(v("n1"), v("kap"), 14.5, A.is_lt, -O1, A.mult)
-    ts(v("k8"), v("kap"), 7.0, A.min)
-    ts(v("nb"), v("n1"), -1024.0, A.mult)
-    ts(v("a1"), v("k8"), -8.0, A.mult, 121.0, A.add)
-    ts(v("a2"), v("k8"), 8.0, A.mult, 24.0, A.add)
-    for h in (0, 1):
-        quant("x0", v("xin", 512 * h, 512 * h + 512), 128, 128 * h)
-        scores(0, h)
-    signs(0)
-    cp(v("la0"), v("nmi"))
-    ts(v("ends1"), v("a1"), v("k8"), A.mult, 128.0, A.add)
-    names(0)
-    signs(1)
-    ts(v("ends2"), v("a2"), v("k8"), A.mult, 15.0, A.add)
-    names(1)
-    name_row(0)
-    scatter(v("w0", 128, 256), v("la0"), v("plc"))
-    name_row(1)
-    wrap(0)
-    wrap(1)
-    wrapped(0)
-    compare(0, "S")
-    compare(0, "V")
-    look_up(0)
-    wrapped(1)
-    for n, c in (("2", 128.0), ("3", 256.0)):
-        act(v("st" + n), v("st1"), F.Copy, scale=c)
-        act(v("n" + n), v("n1"), F.Copy, scale=c)
-    act(v("n2b"), v("n1"), F.Copy, scale=128.0)
-    for m in range(8):
-        act(v("keep", off2(m), off2(m + 1)), v("tm2", 112 - 16 * m, 128), F.Copy)
-    next_use(0)
-    quant("e", v("ctile", 3, 515), 128, 0)
-    steps = places(0)
-    for b in range(1, 4):
-        next(steps, None)
-        quant("e", v("ctile", 3 - b, 515 - b), 128, 128 * b)
-    for m in range(8):
-        act(v("keep", off2(m), off2(m) + 1), v("o16", 0, 1), F.Copy)
-    act(v("cs"), v("n1"), F.Identity, scale=256.0, bias=8192.0)
+    def store_y(t, k):
+        a, e = (256, 384) if k else (0, 256)
+        dma("Y" if k else "S", T.y[:, a:e], T.ysb[:, a:e], v("ysb", a, e)[1], [])
 
-    for t in range(R):
-        if t > 0:
-            new_x(t, 0)
-            scores(t, 0)
-            copy_y(1, (0, 1))
-            signs(0)
-            copy_y(1, (2, 3))
-            decode_x(t, 0, (0, 1, 2))
-            src = sources(t - 1)
-            next(src)
-            names(0)
-            next(src)
-            new_x(t, 1)
-            next(src)
-            scores(t, 1)
-            name_row(0)
-            copy_x(t, 0, (0, 1))
-            decode_x(t, 1, (0, 1))
-            decode_x(t, 0, (3,))
-            signs(1)
-            wrap(0)
-            table(t, 0)
-            decode_x(t, 1, (2, 3))
-            wrapped(0)
-            compare(0, "S")
-            compare(0, "V")
-            names(1)
-            look_up(0)
-            copy_x(t, 0, (2, 3))
-            name_row(1)
-            copy_x(t, 1, range(4))
-            next_use(0)
-            pl = places(0)
-            next(pl)
-            wrap(1)
-            next(pl)
-            wrapped(1)
-            border(t - 1, range(4))
-        else:
-            compare(1, "S")
-        latest(0)
-        if t == 0:
-            quant("f0", v("hin"), 128)
-        compare(1, "V")
-        last_uses(0)
-        wrap_latest(0)
-        if t > 0:
-            send_border(t - 1)
-            compare(1, "S")
-        ranks(0)
-        if t == 0:
-            for h in (0, 1):
-                decode_x(0, h, range(4))
-                copy_x(0, h, range(4))
-        counts(0)
-        next_use(1)
-        count_sums(0)
-        for x in zip(places(1), distance(0)):
-            pass
-        rank_list(t, 0)
-        table(t, 1)
-        look_up(1)
-        hand_on()
-        latest(1)
-        last_uses(1)
-        wrap_latest(1)
-        decode_f(t)
-        copy_f(t)
-        ranks(1)
-        counts(1)
-        count_sums(1)
-        mix(t, 0)
-        run(distance(1))
-        layer(0)
-        rank_list(t, 1)
-        if t < R - 1:
-            send_ranks(t)
-        copy_y(0)
-        mix(t, 1)
-        layer(1)
+    def stores(t, k):
+        a, n, name = (256, 128, "f%d" % R) if k else (0, 256, "x%d" % R)
+        dma("Y", T.oc[:, 4 * a:4 * (a + n)], T["q" + name][:, 0:n].bitcast(dt.uint8), v("q" + name)[1], [])
+        for i in range(4):
+            dma("Y" if i % 2 else "S", T.osc[4 * i:4 * i + 4, a:a + n], T["s" + name][32 * i:32 * i + 4, 0:n], v("s" + name)[1], [])
 
-    new_x(R, 0)
-    decode_x(R, 0, range(4))
-    copy_y(1, (0, 1))
-    run(sources(R - 1))
-    copy_y(1, (2, 3), "V")
-    copy_x(R, 0, range(4))
-    new_x(R, 1)
-    decode_x(R, 1, range(4))
-    copy_x(R, 1, (0, 1))
-    copy_x(R, 1, (2, 3), "V")
-    border(R - 1, (0, 1))
-    border(R - 1, (2, 3), "V")
-    send_border(R - 1)
-    send_ranks(R - 1)
-    quant("v", v("vin"), 128)
-    mm(1, 256, "v", 0, "x3")
-    act(v("ysb", 0, 256), ps(1, 256), F.Copy)
-    act(v("olb", 0, 256), ind(v("iota", 0, 128), v("d16")), F.Identity, bias=127.0, scale=-1.0 / 64)
+    def load(q, name, src, a, e):
+        dma(q, T[name][:, a:e], src[:, a:e], [], v(name, a, e)[1])
 
-    def stores(a, n, q, s):
-        dma("Y", T.oc[:, 4 * a:4 * (a + n)], T[q][:, 0:n].bitcast(dt.uint8), v(q)[1], [])
-        for k in range(4):
-            dma("Y" if k % 2 else "S", T.osc[4 * k:4 * k + 4, a:a + n], T[s][32 * k:32 * k + 4, 0:n], v(s)[1], [])
+    def bitwise(name, c, op):
+        emit("V", lambda: g.vector.tensor_scalar(T[name][:], T.qi[:], c, None, op), v("qi")[1], v(name)[1])
 
-    dma("S", T.y[:, 0:256], T.ysb[:, 0:256], v("ysb", 0, 256)[1], [])
-    stores(0, 256, "qx3", "sx3")
-    mm(2, 128, "v", 0, "f3")
-    cp(v("ysb", 256, 384), ps(2, 128))
-    stores(256, 128, "qf3", "sf3")
-    dma("Y", T.y[:, 256:384], T.ysb[:, 256:384], v("ysb", 256, 384)[1], [])
-    scatter(v("olb", 256, 384), v("la3"), v("nms"))
-    dma("S", T.ol[:, :], T.olb[0:128:16, :], v("olb")[1], [])
+    def segments(name, off, src):
+        for m in range(8):
+            a, e = src(m)
+            act(v(name, off(m), off(m) + e - a), v("tm1" if name == "inc" else "tm2", a, e), F.Copy)
+
+    def line(name, scale, bias=0.0, of="kap"):
+        act(v(name), v(of), F.Identity, scale=scale, bias=bias)
+
+    steps = {
+        "new_x": new_x, "scores": scores, "signs": signs, "names": names, "name_row": name_row, "wrap": wrap, "wrapped": wrapped,
+        "compare": compare, "next_use": next_use, "place": place, "place_list": place_list, "table": table, "look_up": look_up,
+        "hand_on": hand_on, "latest": latest, "wrap_latest": wrap_latest, "counts": counts, "count_sums": count_sums, "distance": distance,
+        "distance_list": distance_list, "decode_f": decode_f, "copy_f": copy_f, "mix": mix, "layer": layer, "copy_y": copy_y,
+        "copy_y_v": copy_y_v, "decode_x": decode_x, "copy_x": copy_x, "copy_x_v": copy_x_v, "last_uses": last_uses, "rank_start": rank_start,
+        "ranks": ranks, "rank_list": rank_list, "send_ranks": send_ranks, "sources": sources, "wrap_sources": wrap_sources,
+        "source_list": source_list, "border": border, "border_v": border_v, "send_border": send_border, "y_x": y_x, "y_f": y_f,
+        "store_y": store_y, "stores": stores,
+        "ol_d": lambda t: act(v("olb", 0, 256), ind(v("iota", 0, 128), v("d16")), F.Identity, bias=127.0, scale=-1.0 / 64),
+        "ol_a": lambda t: scatter(v("olb", 256, 384), v("la%d" % R), v("nms")),
+        "store_ol": lambda t: dma("S", T.ol[:, :], T.olb[0:128:16, :], v("olb")[1], []),
+        "load_x": lambda t, h: load("Y", "xin", T.x, 512 * h, 512 * h + 512),
+        "load_u": lambda t: load("S", "uin", T.u, 0, 512),
+        "load_h": lambda t: load("S", "hin", T.h, 0, 512),
+        "load_v": lambda t: load("Y", "vin", T.v, 0, 512),
+        "load_nm": lambda t: load("Y", "nmi", T.nm, 0, 8),
+        "load_ws": lambda t: load("S", "sw", T.ws, 0, 512),
+        "load_w": lambda t: dma("Y", T.qw[:, 0:512].bitcast(dt.uint8), T.wc[:, 0:2048], [], v("qw")[1]),
+        "quant_u": lambda t: quant("u", v("uin")),
+        "quant_v": lambda t: quant("v", v("vin")),
+        "quant_h": lambda t: quant("f0", v("hin")),
+        "la0": lambda t: cp(v("la0"), v("nmi")),
+        "first_table": lambda t: scatter(v("w0", 128, 256), v("la0"), v("plc")),
+        "lane": lambda t: iota(v("qi"), [[0, 1]], 0, 1, small=False),
+        "lane_low": lambda t: bitwise("qi2", 15, A.bitwise_and),
+        "lane_high": lambda t: bitwise("qi3", 4, A.logical_shift_right),
+        "kap": lambda t: cp(v("kap"), v("qi2")),
+        "grp": lambda t: cp(v("grp"), v("qi3")),
+        "k1": lambda t: ts(v("k1"), v("kap"), 1.0, A.add),
+        "o16": lambda t: iota(v("o16"), [[1, 18]]),
+        "blk": lambda t: iota(v("blk"), [[1, 8], [0, 16]]),
+        "ntile0": lambda t: fill(v("ntile"), 0.0),
+        "bits0": lambda t, h: act(v("bits%d" % h), v("ntile"), F.Copy),
+        "pe16": lambda t: ts(v("pe16"), v("o16", 0, 16), v("kap"), A.is_lt, 1.0, A.add),
+        "pwv": lambda t: scan(v("pwv"), v("pe16"), v("pe16"), -0.5, A.mult, A.min),
+        "pw": lambda t: ts(v("pw"), v("kap"), 6.5, A.is_lt, v("pwv", 15, 16), A.mult),
+        "ntile": lambda t: ts(v("ntile", 0, 512, 4), v("blk"), v("grp"), A.is_equal, v("pw"), A.mult),
+        "quant_n": lambda t: quant("n", v("ntile")),
+        "ones": lambda t: iota(v("ctile"), [[0, 516]], 1),
+        "diagonal": lambda t: keep_where(v("ctile"), [[1, 516]], A.is_equal, -3, -4),
+        "quant_e": lambda t, b: quant("e", v("ctile", 3 - b, 515 - b), 128, 128 * b),
+        "sta": lambda t: ts(v("sta"), v("o16", 0, 16), v("k1"), A.is_equal, O1, A.mult),
+        "stb": lambda t: ts(v("stb"), v("o16", 0, 16), v("kap"), A.is_equal),
+        "st1": lambda t: tt(v("st1", 0, 16), v("sta"), v("stb"), A.add),
+        "st1a": lambda t: act(v("st1", 16, 32), v("st1", 0, 16), F.Copy),
+        "st1b": lambda t: act(v("st1", 32, 64), v("st1", 0, 32), F.Copy),
+        "st1c": lambda t: act(v("st1", 64, 128), v("st1", 0, 64), F.Copy),
+        "st2": lambda t: line("st2", 128.0 / EPS, of="st1"),
+        "st3": lambda t: line("st3", 256.0 / EPS, of="st1"),
+        "n1": lambda t: ts(v("n1"), v("kap"), 14.5, A.is_lt, -O1, A.mult),
+        "n1b": lambda t: line("n1b", 1.0, of="n1"),
+        "m1": lambda t: line("m1", -1.0, of="n1"),
+        "c1": lambda t: line("c1", 1.0, -O1, "n1"),
+        "n2": lambda t: line("n2", 128.0 / EPS, of="n1"),
+        "n2b": lambda t: line("n2b", 128.0 / EPS, of="n1"),
+        "n3": lambda t: line("n3", 256.0 / EPS, of="n1"),
+        "cs": lambda t: line("cs", 256.0 / EPS, 8192.0, "n1"),
+        "tm1": lambda t: fill(v("tm1"), -EPS),
+        "tm1a": lambda t: ts(v("tm1", 0, 18), v("o16"), v("k1"), A.is_equal, 2.0, A.mult),
+        "tm1b": lambda t: ts(v("tm1", 0, 18), v("tm1", 0, 18), -EPS, A.add),
+        "inc": lambda t: segments("inc", off1, lambda m: (0, 129 - 16 * m)),
+        "inc_a": lambda t: act(v("inc", 128, 519, 130), v("tm1", 20, 24), F.Identity, bias=v("m1")),
+        "inc_b": lambda t: act(v("inc", 145, S1, 146), v("tm1", 16, 80, 16), F.Identity, bias=v("m1")),
+        "dummy": lambda t: iota(v("row", 128, 288, 144), [[0, 2]], -1),
+        "tm2": lambda t: fill(v("tm2"), 1.0),
+        "tm2a": lambda t: ts(v("tm2", 112, 128), v("stb"), 63.0, A.mult, 1.0, A.add),
+        "keep": lambda t: segments("keep", off2, lambda m: (112 - 16 * m, 128)),
+        "keep_a": lambda t: act(v("keep", 0, S2, 144), v("tm2", 0, 4), F.Copy, scale=0.0),
+        "keep_b": lambda t: act(v("keep", 16, 497, 160), v("tm2", 0, 4), F.Copy, scale=0.0),
+        "a1": lambda t: line("a1", 130.0, 128.0),
+        "a2": lambda t: line("a2", -146.0, 1167.0),
+        "a3": lambda t: line("a3", 160.0, 15.0),
+        "a4": lambda t: line("a4", -144.0, 1151.0),
+        "ends1": lambda t: ts(v("ends1"), v("a1"), v("a2"), A.min),
+        "ends2": lambda t: ts(v("ends2"), v("a3"), v("a4"), A.min),
+        "iota": lambda t: iota(v("iota"), [[64, 256]]),
+        "plc": lambda t: iota(v("plc"), [[-64, 128]], 64 * 127),
+        "nms": lambda t: iota(v("nms"), [[1, 128]]),
+        "hold0": lambda t: iota(v("hold", 143, 384, 16), [[0, 16]]),
+        "vh0": lambda t: iota(v("vh", 143, 384, 16), [[0, 16]]),
+    }
+    for t, part in enumerate([FIRST] + [ROUND] * (R - 1) + [LAST]):
+        for step in part.split(","):
+            name, *args = step.split()
+            steps[name](t, *[int(a) for a in args])
 
     for s in ("cv", "cs", "cp", "cg"):
         g.wait_ge(T.sem[s], count[s])

from concourse.mybir import dt, AluOpType as A, ActivationFunctionType as F

C, K, R = 256, 128, 3
EPS = 1.0 / 1024
O1 = -128.0 * EPS

FIRST = """load_x 0, load_u, load_x 1, load_nm, load_h, load_w, load_ws, load_v, lane, o16, blk, ntile0, tm1, lane_low, tm2, bits0 0, kap, bits0 1,
ones, diagonal, k1, tm1a, tm1b, sta, stb, pe16, lane_high, st1, pwv, grp, dummy, plc, hold0, iota, vh0, nms, n1, pw, ntile, tm2a, a2, a3,
st1a, a4, m1, st1b, inc, a1, c1, la0, ends2, quant_u, new_x 0, quant_n, st1c, inc_a, scores 0, new_x 1, scores 1, n2b, signs 0, n1b, st2, st3,
quant_e 0, quant_e 1, quant_e 2, names 0, signs 1, first_table, names 1, cs, name_row 0, inc_b, wrap 0, keep, name_row 1, quant_e 3,
compare 0 0, compare 0 1, ends1, wrapped 0, look_up 0, n2, next_use 0, wrap 1, place 0, wrapped 1, place_list 0, decode_x 0 0 1 2 3,
copy_x 0 0, copy_x 0 1, copy_x 0 2, copy_x 0 3, decode_x 1 0 1 2 3, latest 0, last_uses 0, quant_h, copy_x 1 0, copy_x 1 1, compare 1 0,
compare 1 1, wrap_latest 0, rank_start 0, keep_a, ranks 0 0, ranks 0 1, keep_b, next_use 1, counts 0 1, counts 0 0, place 1, rank_list 0,
quant_v, count_sums 0, distance 0, place_list 1, hand_on, table 1, look_up 1, copy_x 1 2, copy_x 1 3, n3, distance_list 0, latest 1,
wrap_latest 1, last_uses 1, decode_f, copy_f 0, copy_f 1, copy_f 2, rank_start 1, copy_f 3, ranks 1 0, ranks 1 1, counts 1 1, counts 1 0,
mix 0 0, count_sums 1, mix 0 1, mix 0 2, mix 0 3, distance 1, layer 0, distance_list 1, rank_list 1, send_ranks, copy_y 0 0, copy_y 0 1,
copy_y 0 2, copy_y 0 3, mix 1 0, mix 1 1, mix 1 2, mix 1 3, layer 1"""
ROUND = """new_x 0, scores 0, copy_y 1 0, copy_y 1 1, copy_y 1 2, signs 0, decode_x 0 0 1, decode_x 0 2, sources, copy_y_v 1 3, wrap_sources,
names 0, new_x 1, source_list, scores 1, copy_x 0 0, copy_x 0 1, decode_x 1 0 1, copy_x 0 2, name_row 0, decode_x 0 3, signs 1, wrap 0,
decode_x 1 2, compare 0 1, names 1, decode_x 1 3, copy_x 1 0, copy_x 1 1, border 0, border 1, table 0, compare 0 0, wrapped 0, name_row 1,
look_up 0, copy_x 0 3, copy_x 1 3, copy_x 1 2, next_use 0, place 0, place_list 0, wrap 1, border 3, border 2, latest 0, last_uses 0,
compare 1 1, send_border, wrapped 1, compare 1 0, wrap_latest 0, rank_start 0, ranks 0 0, ranks 0 1, counts 0 1, counts 0 0, next_use 1,
rank_list 0, count_sums 0, place 1, distance 0, place_list 1, distance_list 0, hand_on, table 1, look_up 1, latest 1, wrap_latest 1,
last_uses 1, decode_f, rank_start 1, copy_f 0, copy_f 1, copy_f 2, copy_f 3, ranks 1 0, ranks 1 1, counts 1 1, counts 1 0, count_sums 1,
mix 0 0, mix 0 1, mix 0 2, distance 1, mix 0 3, distance_list 1, layer 0, copy_y 0 1, copy_y 0 2, mix 1 0, mix 1 1, mix 1 2, mix 1 3,
rank_list 1, send_ranks, copy_y 0 0, copy_y 0 3, layer 1"""
LAST = """sources, new_x 0, decode_x 0 0 1 2 3, copy_y 1 0, copy_y 1 1, copy_y_v 1 2, copy_y_v 1 3, copy_x 0 0, copy_x 0 1, copy_x 0 2, copy_x 0 3,
new_x 1, wrap_sources, source_list, decode_x 1 0 1 2 3, copy_x 1 0, copy_x 1 1, copy_x_v 1 2, copy_x_v 1 3, border 0, border 1, border_v 2,
border_v 3, send_border, y_x, ol_d, store_y 0, stores 0, ol_a, store_ol, y_f, stores 1, store_y 1"""


def off1(m):
    return 146 * m if m < 4 else 146 * (7 - m) + 17 + 16 * m


def off2(m):
    return 144 * m if m < 4 else 144 * (7 - m) + 128 - 16 * m


S1, S2 = 4 * 146, 4 * 144
BF, F32, I32, U16, U8, Q8 = "bfloat16", "float32", "int32", "uint16", "uint8", "float8_e4m3fn_x4"
SCRATCH, TINY = {}, {}


def buf(name, n, d=BF, where="sbuf"):
    SCRATCH[name] = (where, [128, n], d)


for _n, _w in (("xin", 1024), ("hin", 512), ("uin", 512), ("vin", 512), ("bits0", 512), ("bits1", 512), ("ctile", 516), ("ntile", 512),
               ("zt", 1024), ("yt", 1024), ("blk", 128), ("o16", 18), ("pe16", 16), ("st1", 128), ("st2", 128), ("st3", 128),
               ("sta", 16), ("stb", 16), ("tm1", 130), ("tm2", 128), ("inc", S1), ("keep", S2), ("iota", 256), ("plc", 128), ("nms", 128),
               ("row", 288), ("hold", 384), ("qq0", S1), ("qq1", S1), ("sc0", S1), ("sc1", S1), ("w0", 256), ("w1", 256), ("r1", 128),
               ("vh", 384), ("lh0", 128), ("lt0", S2), ("lt1", S2), ("cs0", S2), ("cs1", S2), ("junk", 512), ("srow", 128), ("gx", 1536),
               ("n1b", 1), ("n2b", 1)):
    buf(_n, _w)
for _n, _w in (("kap", 1), ("grp", 1), ("pw", 1), ("k1", 1), ("a1", 1), ("a2", 1), ("a3", 1), ("a4", 1), ("n1", 1), ("n2", 1), ("n3", 1), ("m1", 1),
               ("c1", 1), ("cs", 1), ("pwv", 16), ("x0", 16), ("x1", 16), ("y0", 16), ("y1", 16), ("lw0", 8), ("lw1", 8), ("acc0", 8), ("acc1", 8)):
    TINY[_n] = (sum(w for o, w in TINY.values()), _w)
buf("tiny", sum(w for o, w in TINY.values()), F32)
for _n, _w in (("ysb", 384), ("olb", 384), ("lh1", 128), ("sh", 128)):
    buf(_n, _w, F32)
for _n, _w in (("qi", 1), ("qi2", 1), ("qi3", 1), ("nmi", 8)):
    buf(_n, _w, I32)
for _n, _w in (("ends1", 1), ("ends2", 1), ("nw16", 16), ("off16", 16), ("d16", 16), ("src16", 8), ("la0", 8), ("lm", 8)):
    buf(_n, _w, U16)
for _t in range(R):
    buf("g%d" % _t, 1536)
    buf("bt%d" % _t, 512)
    buf("sa%d" % _t, 8, U16)
    buf("la%d" % (_t + 1), 8, U16)
    buf("qb%d" % _t, 128, Q8)
    buf("sb%d" % _t, 128, U8)
for _n, _w in (("u", 128), ("v", 128), ("w", 512), ("e", 512), ("n", 128), ("bit0", 128), ("bit1", 128), ("z", 256),
               ("x0", 256), ("x1", 256), ("x2", 256), ("x3", 256), ("f0", 128), ("f1", 128), ("f2", 128), ("f3", 128)):
    buf("q" + _n, _w, Q8)
    buf("s" + _n, _w, U8)
for _n in range(8):
    buf("p%d" % _n, 512, F32, "psum")

NDMA = 21
SEMAPHORES = ["cv", "cs", "cp", "cg", "left"] + ["ra%d" % t for t in range(R)] + ["rb%d" % t for t in range(R)] + ["d%d" % i for i in range(NDMA)]


def rank_program(g, core, T, topo):
    rank = T.rank_of(core)
    if rank is None:
        return
    queues = {"V": g.vector, "S": g.scalar, "P": g.tensor, "G": g, "Y": g.sync}
    semof = {"V": "cv", "S": "cs", "P": "cp", "G": "cg"}
    count = {"cv": 0, "cs": 0, "cp": 0, "cg": 0}
    seen = {q: {} for q in queues}
    hist, dmas, left, turn = {}, [0], [0], [0]

    def wait(q, needs):
        for s in sorted(needs):
            if seen[q].get(s, 0) < needs[s]:
                queues[q].wait_ge(T.sem[s], needs[s])
                seen[q][s] = needs[s]

    def need_of(q, reads, writes):
        needs = {}
        for refs, wr in ((reads, False), (writes, True)):
            for name, lo, hi, *ph in refs:
                psum = SCRATCH[name][0] == "psum"
                for l, h, w, q2, s, n, *ph2 in hist.get(name, []):
                    if l < hi and lo < h and (w or wr or (psum and q2 != q)) and not (ph and ph2 and ph != ph2):
                        needs[s] = max(needs.get(s, 0), n)
        return needs

    def note(q, reads, writes, s, n):
        for name, lo, hi, *ph in writes:
            hist[name] = [r for r in hist.get(name, []) if not (lo <= r[0] and r[1] <= hi and (not ph or list(r[6:]) == ph))] + [(lo, hi, True, q, s, n, *ph)]
        for name, lo, hi, *ph in reads:
            hist[name] = [r for r in hist.get(name, []) if r[2] or r[3] != q or not (lo <= r[0] and r[1] <= hi)] + [(lo, hi, False, q, s, n)]

    def emit(q, fn, reads, writes):
        wait(q, need_of(q, reads, writes))
        s = semof[q]
        count[s] += 1
        fn().then_inc(T.sem[s], 1)
        note(q, reads, writes, s, count[s])

    def dma(q, o, i, reads, writes):
        wait(q, need_of(q, reads, writes))
        s = "d%d" % dmas[0]
        dmas[0] += 1
        queues[q].dma_start(o, i).then_inc(T.sem[s], 16)
        note(q + "d", reads, writes, s, 16)

    def v(name, a=0, b=None, st=None):
        if name in TINY:
            o, n = TINY[name]
            return v("tiny", o + a, o + (n if b is None else b), st)
        b = SCRATCH[name][1][1] if b is None else b
        view = T[name][:, a:b] if st is None else T[name][:, a:b:st]
        return view, [(name, a, b) if st != 4 else (name, a, b, a % 4)]

    def ps(bank, n):
        return T["p%d" % bank][:, 0:n], [("p%d" % bank, 0, 512)]

    def ind(win, lst):
        return win[0].indirect(lst[0]), win[1] + lst[1]

    def tt(o, a, b, op):
        emit("V", lambda: g.vector.tensor_tensor(o[0], a[0], b[0], op), a[1] + b[1], o[1])

    def ts(o, a, s1, op0, s2=None, op1=None):
        r, x = list(a[1]), [s1, s2]
        for i in (0, 1):
            if isinstance(x[i], tuple):
                r += x[i][1]
                x[i] = x[i][0]
        if op1 is None:
            emit("V", lambda: g.vector.tensor_scalar(o[0], a[0], x[0], None, op0), r, o[1])
        else:
            emit("V", lambda: g.vector.tensor_scalar(o[0], a[0], x[0], x[1], op0, op1), r, o[1])

    def cp(o, a):
        emit("V", lambda: g.vector.tensor_copy(o[0], a[0]), a[1], o[1])

    def scatter(win, lst, a):
        emit("V", lambda: g.vector.tensor_copy(win[0].indirect(lst[0]), a[0]), a[1] + lst[1], win[1])

    def scan(o, d0, d1, init, op0, op1):
        emit("V", lambda: g.vector.tensor_tensor_scan(o[0], d0[0], d1[0], init, op0, op1), d0[1] + d1[1], o[1])

    def fill(o, c):
        emit("V", lambda: g.vector.memset(o[0], c), [], o[1])

    def act(o, a, func, bias=None, scale=1.0, acc=None):
        r, w, kw = list(a[1]), list(o[1]), {"scale": scale}
        if isinstance(bias, tuple):
            kw["bias"] = bias[0]
            r += bias[1]
        elif bias is not None:
            kw["bias"] = bias
        if acc is not None:
            kw["accum_out"] = acc[0]
            w += acc[1]
        emit("S", lambda: g.scalar.activation(o[0], a[0], func, **kw), r, w)

    def quant(name, src, n=128, a=0):
        q, s = v("q" + name, a, a + n), v("s" + name, a, a + n)
        emit("V", lambda: g.vector.quantize_mx(q[0], s[0], src[0]), src[1], q[1] + s[1])

    def mm(bank, n, l, la, r, ra=0):
        o = ps(bank, n)
        lq, ls = v("q" + l, la, la + 128), v("s" + l, la, la + 128)
        rq, rs = v("q" + r, ra, ra + n), v("s" + r, ra, ra + n)
        emit("P", lambda: g.tensor.matmul_mx(o[0], lq[0], ls[0], rq[0], rs[0], True, True), lq[1] + ls[1] + rq[1] + rs[1], o[1])

    def iota(o, pattern, base=0, cm=0, small=True):
        if small:
            emit("G", lambda: g.iota(o[0], pattern, base, cm, allow_small_or_imprecise_dtypes=True), [], o[1])
        else:
            emit("G", lambda: g.iota(o[0], pattern, base, cm), [], o[1])

    def keep_where(o, pattern, op, base, cm):
        emit("G", lambda: g.affine_select(o[0], o[0], pattern, op, 0.0, base, cm), o[1], o[1])

    def junk():
        turn[0] = (turn[0] + 1) % 4
        return v("junk", 128 * turn[0], 128 * turn[0] + 128)

    nxt = T.cores[(rank + 1) % len(T.cores)]
    rid, pid = topo.addr(nxt, core)
    eng = topo.engines(core, nxt)[:8]
    mask = sum(1 << e for e in eng)

    def send(dst, src, rsem, reads):
        wait("G", need_of("G", reads, []))
        g.remote_dma(dst, src, T.sem[rsem], T.sem.left, pid, rid, mask)
        left[0] += len(eng)

    def x_of(t, b, h):
        return v("gx" if t == 0 else "g%d" % (t - 1), 384 * b + 128 + 128 * h, 384 * b + 256 + 128 * h)

    def front_of(t, b):
        return v("g%d" % t, 384 * b, 384 * b + 128)

    def held(name, h, n=8):
        return v(name, 128 * h + 15, 128 * h + 16 * n, 16)

    def new_x(t, h):
        quant("x%d" % t, v("yt" if t else "xin", 512 * h, 512 * h + 512), 128, 128 * h)

    def scores(t, h):
        mm(4 * h, 128, "u", 0, "x%d" % t, 128 * h)

    def signs(t, h):
        act(v("bits%d" % h, 0, 512, 4), ps(4 * h, 128), F.Sign, bias=2.0 ** -100)

    def names(t, h):
        quant("bit%d" % h, v("bits%d" % h))
        mm(4 * h + 1, 128, "n", 0, "bit%d" % h)

    def name_row(t, h):
        act(v("row", 144 * h, 144 * h + 128), ps(4 * h + 1, 128), F.Identity, bias=63.5 * EPS, scale=EPS)

    def wrap(t, h):
        scan(v("hold", 128 * h, 128 * h + 128), v("st1"), v("row", 144 * h, 144 * h + 128), 0.0, A.add, A.min)

    def wrapped(t, h):
        ts(v("nw16", 8 * h, 8 * h + 8), held("hold", h), v("n1"), A.add, 1 / EPS, A.mult)

    def compare(t, h, k):
        for m in range(4 * k, 4 * k + 4):
            c = 128 * h + 16 * m + 15
            ts(v("qq%d" % h, off1(m), off1(m) + 129 - 16 * m), v("row", 144 * h + 16 * m, 144 * h + 129), v("n1b"), A.subtract,
               v("hold", c, c + 1), A.not_equal)

    def next_use(t, h):
        scan(v("sc%d" % h), v("inc"), v("qq%d" % h), 0.0, A.add, A.min)

    def place(t, h):
        tt(v("x%d" % h), ind(v("sc%d" % h), v("ends1")), held("hold", h, 16), A.min)

    def place_list(t, h):
        ts(v("off16", 8 * h, 8 * h + 8), v("x%d" % h, 0, 8), v("c1"), A.add, 1 / EPS, A.mult)

    def table(t, h):
        act(v("r1") if h else v("w0", 128, 256), ind(v("iota", 0, 128), v("lm" if h else "la%d" % t)), F.Copy)

    def look_up(t, h):
        act(v("w%d" % h, 0, 128), ind(v("r1") if h else v("w0", 128, 256), v("nw16", 8 * h, 8 * h + 8)), F.Copy)

    def hand_on(t):
        act(v("w1", 128, 256), v("w0", 128, 256), F.Identity, bias=-8192.0)

    def latest(t, h):
        scatter(v("w%d" % h), v("off16", 8 * h, 8 * h + 8), v("iota", 128, 256))

    def wrap_latest(t, h):
        scan(v("vh", 128 * h, 128 * h + 128), v("st2"), v("w%d" % h, 0, 128), 0.0, A.add, A.min)

    def counts(t, h, k):
        for m in range(4 * k, 4 * k + 4):
            c = 128 * h + 16 * m + 15
            ts(v("lt%d" % h, off2(m), off2(m) + 16 * m + 16), v("w%d" % h, 0, 16 * m + 16), v("n2b"), A.subtract, v("vh", c, c + 1), A.is_lt)

    def count_sums(t, h):
        scan(v("cs%d" % h), v("keep"), v("lt%d" % h), 0.0, A.mult, A.add)

    def distance(t, h):
        tt(v("y%d" % h), ind(v("cs%d" % h), v("ends2")), held("vh", h, 16), A.subtract)

    def distance_list(t, h):
        ts(v("d16", 8 * h, 8 * h + 8), v("y%d" % h, 0, 8), v("n2"), A.subtract, -1.0 / 64, A.mult)

    def decode_f(t):
        for b in range(4):
            mm(b, 128, "e", 128 * b, "f%d" % t)

    def copy_f(t, b):
        i = ps(b, 128) if t else (T["p%d" % b][:, 127::-1], ps(b, 128)[1])
        act(front_of(t, b), i, F.Copy, scale=0.5)

    def mix(t, h, b):
        tt(v("zt", 512 * h + b, 512 * h + 512, 4), ind(front_of(t, b), v("d16", 8 * h, 8 * h + 8)), x_of(t, b, h), A.add)

    def layer(t, h):
        quant("z", v("zt", 512 * h, 512 * h + 512), 128, 128 * h)
        for b in range(4):
            mm(4 * h + b, 128, "w", 128 * b, "z", 128 * h)

    def copy_y(t, h, b):
        act(v("yt", 512 * h + b, 512 * h + 512, 4), ps(4 * h + b, 128), F.Copy, scale=0.03125)

    def copy_y_v(t, h, b):
        ts(v("yt", 512 * h + b, 512 * h + 512, 4), ps(4 * h + b, 128), 0.03125, A.mult)

    def xbank(h, b):
        return ((2, 3, 0, 1), (6, 7, 4, 2))[h][b]

    def decode_x(t, h, *planes):
        for b in planes:
            mm(xbank(h, b), 128, "e", 128 * b, "x%d" % t, 128 * h)

    def copy_x(t, h, b):
        act(x_of(t, b, h), ps(xbank(h, b), 128), F.Copy, scale=0.5)

    def copy_x_v(t, h, b):
        ts(x_of(t, b, h), ps(xbank(h, b), 128), 0.5, A.mult)

    def last_uses(t, h):
        scan(v("lh%d" % h), v("st3" if h else "st2"), v("w%d" % h, 128, 256), 0.0, A.add, A.min)

    def rank_start(t, h):
        act(v("lw%d" % h), held("lh%d" % h, 0), F.Identity, bias=v("n3" if h else "n2"))

    def ranks(t, h, k):
        for m in range(4 * k, 4 * k + 4):
            act(junk(), v("w%d" % h, 128, 256), F.Sign, bias=v("lw%d" % h, m, m + 1), scale=-1.0, acc=v("acc%d" % h, m, m + 1))

    def rank_list(t, h):
        ts(v("sa%d" % t if h else "lm"), v("acc%d" % h), 0.5 if t < R - 1 or not h else -0.5, A.mult, 63.5, A.add)

    def send_ranks(t):
        send(T["la%d" % (t + 1)][:], T["sa%d" % t][:], "ra%d" % t, v("sa%d" % t)[1])
        hist["la%d" % (t + 1)] = [(0, 8, True, "R", "ra%d" % t, len(eng))]

    def sources(t):
        scatter(v("srow"), v("sa%d" % (t - 1)), v("w1", 128, 256))

    def wrap_sources(t):
        scan(v("sh"), v("st3"), v("srow"), 0.0, A.add, A.min)

    def source_list(t):
        ts(v("src16"), held("sh", 0), v("cs"), A.add, 1.0 / 64, A.mult)

    def border(t, b):
        act(v("bt%d" % (t - 1), b, 512, 4), ind(v("g%d" % (t - 1), 384 * b, 384 * b + 384), v("src16")), F.Copy, scale=2.0)

    def border_v(t, b):
        ts(v("bt%d" % (t - 1), b, 512, 4), ind(v("g%d" % (t - 1), 384 * b, 384 * b + 384), v("src16")), 2.0, A.mult)

    def send_border(t):
        b, f = "b%d" % (t - 1), "f%d" % t
        quant(b, v("bt%d" % (t - 1)))
        send(T["q" + f][:, 0:128].bitcast(dt.uint8), T["q" + b][:, 0:128].bitcast(dt.uint8), "r" + b, v("q" + b)[1])
        send(T["s" + f][:], T["s" + b][:], "r" + b, v("s" + b)[1])
        for n in ("q" + f, "s" + f):
            hist[n] = [(0, 128, True, "R", "r" + b, 2 * len(eng))]

    def y_x(t):
        mm(1, 256, "v", 0, "x%d" % R)
        act(v("ysb", 0, 256), ps(1, 256), F.Copy)

    def y_f(t):
        mm(2, 128, "v", 0, "f%d" % R)
        cp(v("ysb", 256, 384), ps(2, 128))

    def store_y(t, k):
        a, e = (256, 384) if k else (0, 256)
        dma("Y" if k else "S", T.y[:, a:e], T.ysb[:, a:e], v("ysb", a, e)[1], [])

    def stores(t, k):
        a, n, name = (256, 128, "f%d" % R) if k else (0, 256, "x%d" % R)
        dma("Y", T.oc[:, 4 * a:4 * (a + n)], T["q" + name][:, 0:n].bitcast(dt.uint8), v("q" + name)[1], [])
        for i in range(4):
            dma("Y" if i % 2 else "S", T.osc[4 * i:4 * i + 4, a:a + n], T["s" + name][32 * i:32 * i + 4, 0:n], v("s" + name)[1], [])

    def load(q, name, src, a, e):
        dma(q, T[name][:, a:e], src[:, a:e], [], v(name, a, e)[1])

    def bitwise(name, c, op):
        emit("V", lambda: g.vector.tensor_scalar(T[name][:], T.qi[:], c, None, op), v("qi")[1], v(name)[1])

    def segments(name, off, src):
        for m in range(8):
            a, e = src(m)
            act(v(name, off(m), off(m) + e - a), v("tm1" if name == "inc" else "tm2", a, e), F.Copy)

    def line(name, scale, bias=0.0, of="kap"):
        act(v(name), v(of), F.Identity, scale=scale, bias=bias)

    steps = {
        "new_x": new_x, "scores": scores, "signs": signs, "names": names, "name_row": name_row, "wrap": wrap, "wrapped": wrapped,
        "compare": compare, "next_use": next_use, "place": place, "place_list": place_list, "table": table, "look_up": look_up,
        "hand_on": hand_on, "latest": latest, "wrap_latest": wrap_latest, "counts": counts, "count_sums": count_sums, "distance": distance,
        "distance_list": distance_list, "decode_f": decode_f, "copy_f": copy_f, "mix": mix, "layer": layer, "copy_y": copy_y,
        "copy_y_v": copy_y_v, "decode_x": decode_x, "copy_x": copy_x, "copy_x_v": copy_x_v, "last_uses": last_uses, "rank_start": rank_start,
        "ranks": ranks, "rank_list": rank_list, "send_ranks": send_ranks, "sources": sources, "wrap_sources": wrap_sources,
        "source_list": source_list, "border": border, "border_v": border_v, "send_border": send_border, "y_x": y_x, "y_f": y_f,
        "store_y": store_y, "stores": stores,
        "ol_d": lambda t: act(v("olb", 0, 256), ind(v("iota", 0, 128), v("d16")), F.Identity, bias=127.0, scale=-1.0 / 64),
        "ol_a": lambda t: scatter(v("olb", 256, 384), v("la%d" % R), v("nms")),
        "store_ol": lambda t: dma("S", T.ol[:, :], T.olb[0:128:16, :], v("olb")[1], []),
        "load_x": lambda t, h: load("Y", "xin", T.x, 512 * h, 512 * h + 512),
        "load_u": lambda t: load("S", "uin", T.u, 0, 512),
        "load_h": lambda t: load("S", "hin", T.h, 0, 512),
        "load_v": lambda t: load("Y", "vin", T.v, 0, 512),
        "load_nm": lambda t: load("Y", "nmi", T.nm, 0, 8),
        "load_ws": lambda t: load("S", "sw", T.ws, 0, 512),
        "load_w": lambda t: dma("Y", T.qw[:, 0:512].bitcast(dt.uint8), T.wc[:, 0:2048], [], v("qw")[1]),
        "quant_u": lambda t: quant("u", v("uin")),
        "quant_v": lambda t: quant("v", v("vin")),
        "quant_h": lambda t: quant("f0", v("hin")),
        "la0": lambda t: cp(v("la0"), v("nmi")),
        "first_table": lambda t: scatter(v("w0", 128, 256), v("la0"), v("plc")),
        "lane": lambda t: iota(v("qi"), [[0, 1]], 0, 1, small=False),
        "lane_low": lambda t: bitwise("qi2", 15, A.bitwise_and),
        "lane_high": lambda t: bitwise("qi3", 4, A.logical_shift_right),
        "kap": lambda t: cp(v("kap"), v("qi2")),
        "grp": lambda t: cp(v("grp"), v("qi3")),
        "k1": lambda t: ts(v("k1"), v("kap"), 1.0, A.add),
        "o16": lambda t: iota(v("o16"), [[1, 18]]),
        "blk": lambda t: iota(v("blk"), [[1, 8], [0, 16]]),
        "ntile0": lambda t: fill(v("ntile"), 0.0),
        "bits0": lambda t, h: act(v("bits%d" % h), v("ntile"), F.Copy),
        "pe16": lambda t: ts(v("pe16"), v("o16", 0, 16), v("kap"), A.is_lt, 1.0, A.add),
        "pwv": lambda t: scan(v("pwv"), v("pe16"), v("pe16"), -0.5, A.mult, A.min),
        "pw": lambda t: ts(v("pw"), v("kap"), 6.5, A.is_lt, v("pwv", 15, 16), A.mult),
        "ntile": lambda t: ts(v("ntile", 0, 512, 4), v("blk"), v("grp"), A.is_equal, v("pw"), A.mult),
        "quant_n": lambda t: quant("n", v("ntile")),
        "ones": lambda t: iota(v("ctile"), [[0, 516]], 1),
        "diagonal": lambda t: keep_where(v("ctile"), [[1, 516]], A.is_equal, -3, -4),
        "quant_e": lambda t, b: quant("e", v("ctile", 3 - b, 515 - b), 128, 128 * b),
        "sta": lambda t: ts(v("sta"), v("o16", 0, 16), v("k1"), A.is_equal, O1, A.mult),
        "stb": lambda t: ts(v("stb"), v("o16", 0, 16), v("kap"), A.is_equal),
        "st1": lambda t: tt(v("st1", 0, 16), v("sta"), v("stb"), A.add),
        "st1a": lambda t: act(v("st1", 16, 32), v("st1", 0, 16), F.Copy),
        "st1b": lambda t: act(v("st1", 32, 64), v("st1", 0, 32), F.Copy),
        "st1c": lambda t: act(v("st1", 64, 128), v("st1", 0, 64), F.Copy),
        "st2": lambda t: line("st2", 128.0 / EPS, of="st1"),
        "st3": lambda t: line("st3", 256.0 / EPS, of="st1"),
        "n1": lambda t: ts(v("n1"), v("kap"), 14.5, A.is_lt, -O1, A.mult),
        "n1b": lambda t: line("n1b", 1.0, of="n1"),
        "m1": lambda t: line("m1", -1.0, of="n1"),
        "c1": lambda t: line("c1", 1.0, -O1, "n1"),
        "n2": lambda t: line("n2", 128.0 / EPS, of="n1"),
        "n2b": lambda t: line("n2b", 128.0 / EPS, of="n1"),
        "n3": lambda t: line("n3", 256.0 / EPS, of="n1"),
        "cs": lambda t: line("cs", 256.0 / EPS, 8192.0, "n1"),
        "tm1": lambda t: fill(v("tm1"), -EPS),
        "tm1a": lambda t: ts(v("tm1", 0, 18), v("o16"), v("k1"), A.is_equal, 2.0, A.mult),
        "tm1b": lambda t: ts(v("tm1", 0, 18), v("tm1", 0, 18), -EPS, A.add),
        "inc": lambda t: segments("inc", off1, lambda m: (0, 129 - 16 * m)),
        "inc_a": lambda t: act(v("inc", 128, 519, 130), v("tm1", 20, 24), F.Identity, bias=v("m1")),
        "inc_b": lambda t: act(v("inc", 145, S1, 146), v("tm1", 16, 80, 16), F.Identity, bias=v("m1")),
        "dummy": lambda t: iota(v("row", 128, 288, 144), [[0, 2]], -1),
        "tm2": lambda t: fill(v("tm2"), 1.0),
        "tm2a": lambda t: ts(v("tm2", 112, 128), v("stb"), 63.0, A.mult, 1.0, A.add),
        "keep": lambda t: segments("keep", off2, lambda m: (112 - 16 * m, 128)),
        "keep_a": lambda t: act(v("keep", 0, S2, 144), v("tm2", 0, 4), F.Copy, scale=0.0),
        "keep_b": lambda t: act(v("keep", 16, 497, 160), v("tm2", 0, 4), F.Copy, scale=0.0),
        "a1": lambda t: line("a1", 130.0, 128.0),
        "a2": lambda t: line("a2", -146.0, 1167.0),
        "a3": lambda t: line("a3", 160.0, 15.0),
        "a4": lambda t: line("a4", -144.0, 1151.0),
        "ends1": lambda t: ts(v("ends1"), v("a1"), v("a2"), A.min),
        "ends2": lambda t: ts(v("ends2"), v("a3"), v("a4"), A.min),
        "iota": lambda t: iota(v("iota"), [[64, 256]]),
        "plc": lambda t: iota(v("plc"), [[-64, 128]], 64 * 127),
        "nms": lambda t: iota(v("nms"), [[1, 128]]),
        "hold0": lambda t: iota(v("hold", 143, 384, 16), [[0, 16]]),
        "vh0": lambda t: iota(v("vh", 143, 384, 16), [[0, 16]]),
    }
    for t, part in enumerate([FIRST] + [ROUND] * (R - 1) + [LAST]):
        for step in part.split(","):
            name, *args = step.split()
            steps[name](t, *[int(a) for a in args])

    for s in ("cv", "cs", "cp", "cg"):
        g.wait_ge(T.sem[s], count[s])
    for i in range(dmas[0]):
        g.wait_ge(T.sem["d%d" % i], 16)
    for i in range(R):
        g.wait_ge(T.sem["ra%d" % i], len(eng))
        g.wait_ge(T.sem["rb%d" % i], 2 * len(eng))
    g.wait_ge(T.sem.left, left[0])
